import numpy as np
import ml_dtypes


def mxq(x, axis, fmt="e4m3"):
    dtype, down = {"e4m3": (ml_dtypes.float8_e4m3fn, 7), "e5m2": (ml_dtypes.float8_e5m2, 14)}[fmt]
    v = np.moveaxis(np.asarray(x, np.float32).astype(ml_dtypes.bfloat16).astype(np.float64), axis, -1)
    blocks = v.reshape(v.shape[:-1] + (-1, 32))
    amax = np.abs(blocks).max(-1, keepdims=True)
    byte = np.maximum(np.where(amax > 0, np.frexp(amax)[1] - 1 + 127, 0) - down, 1)
    scale = np.exp2(byte - 127.0)
    codes = (blocks / scale).astype(np.float32).astype(dtype).astype(np.float64)
    return np.moveaxis((codes * scale).reshape(v.shape), -1, axis)


WIDE = False


def mx_kscale(k):
    if not WIDE:
        return np.ones(k)
    levels = np.array([10, -10, 5, -5, 0])
    if k % 512:
        return np.exp2(np.random.permutation(np.resize(levels, k // 32))).repeat(32)
    a = np.empty((k // 512, 16))
    for p in range(k // 512):
        a[p, :8] = np.random.permutation(np.resize(levels, 8))
        for g in range(8):
            far = levels[np.abs(levels - a[p, g]) >= 10]
            a[p, g + 8] = far[np.random.randint(len(far))]
    return np.exp2(a.ravel()).repeat(32)


BF16 = ml_dtypes.bfloat16


def bf(x):
    return np.asarray(x, np.float32).astype(BF16)


def f64(x):
    return np.asarray(x).astype(np.float64)


E2M1 = np.array([0.0, 0.5, 1.0, 1.5, 2.0, 3.0, 4.0, 6.0, -0.0, -0.5, -1.0, -1.5, -2.0, -3.0, -4.0, -6.0])


def pack_weight(w, fmt):
    k, n = w.shape
    w = f64(bf(w)).reshape(k // 32, 32, n)
    amax = np.abs(w).max(1)
    if fmt == "e4m3":
        byte = np.frexp(amax)[1] - 1 + 127 - 7
    else:
        mant, ex = np.frexp(amax / 6.0)
        byte = np.where(mant > 0.5, ex, ex - 1) + 127
    byte = np.clip(np.where(amax > 0, byte, 1), 1, 254)
    scaled = (w * np.exp2(127.0 - byte)[:, None, :]).reshape(k, n).astype(np.float32)
    by_word = np.ascontiguousarray(scaled.reshape(k // 512, 128, 4, n).transpose(0, 1, 3, 2))
    if fmt == "e4m3":
        words = by_word.astype(ml_dtypes.float8_e4m3fn).view(np.uint8)
    else:
        c = by_word.astype(ml_dtypes.float4_e2m1fn).view(np.uint8) & 0xF
        words = c[..., 0::2] | (c[..., 1::2] << 4)
    return np.ascontiguousarray(words), np.ascontiguousarray(byte.astype(np.uint8).reshape(k // 512, 16, n))


def unpack_weight(words, scales, fmt):
    g, p, n, _ = words.shape
    if fmt == "e4m3":
        vals = np.ascontiguousarray(words).view(ml_dtypes.float8_e4m3fn).astype(np.float64)
    else:
        nib = np.empty((g, p, n, 4), np.uint8)
        nib[..., 0::2] = words & 0xF
        nib[..., 1::2] = words >> 4
        vals = E2M1[nib]
    vals = vals * np.repeat(np.exp2(scales.astype(np.float64) - 127.0), 8, axis=1)[..., None]
    return vals.transpose(0, 1, 3, 2).reshape(g * 512, n)
def pack4(w):
    words, scales = pack_weight(w, "e2m1")
    return words.reshape(words.shape[0], 128, -1), scales


def unpack4(words, scales):
    return unpack_weight(words.reshape(words.shape[0], 128, -1, 2), scales, "e2m1")


M, C, F, I = 1024, 512, 1536, 1024


def draw0():
    s, t, u = mx_kscale(C), mx_kscale(F), mx_kscale(M)
    r = np.random.standard_normal((M, C)) * s * u[:, None]
    w2t = np.random.standard_normal((C, F)) / np.sqrt(C) / s[:, None] * t
    d = 1 - np.tanh(np.random.standard_normal((M, F))) ** 2
    x = np.random.standard_normal((M, I)) / np.sqrt(M) / u[:, None]
    w1t_words, w1t_scales = pack4(np.random.standard_normal((F, I)) / np.sqrt(F) / t[:, None])
    v = np.random.standard_normal((I, F)) * t
    lam = 0.3 + 0.3 * np.random.random(I)
    return {"r": bf(r), "w2t": bf(w2t), "d": bf(d), "x": bf(x),
            "w1t_words": w1t_words, "w1t_scales": w1t_scales,
            "v": bf(v), "lam": bf(lam)}


def core(r, w2t, d, x, w1t_words, w1t_scales, v, lam):
    dh = (mxq(f64(r), 1, "e4m3") @ mxq(f64(w2t), 0, "e4m3")) * f64(d)
    dx = mxq(dh, 1, "e4m3") @ unpack4(w1t_words, w1t_scales)
    gv = mxq(f64(x), 0, "e4m3").T @ mxq(dh, 0, "e4m3")
    return dx, gv + f64(lam)[:, None] * f64(v)


def e4m3fn_bytes(y):
    return np.clip(np.asarray(y, np.float64), -448.0, 448.0).astype(np.float32).astype(ml_dtypes.float8_e4m3fn).view(np.uint8)


def e4m3fn_values(b):
    return np.asarray(b, np.uint8).view(ml_dtypes.float8_e4m3fn).astype(np.float64)


def setup_inputs():
    d = draw0()
    x0 = np.asarray(d['x']).astype(np.float64)
    s = (np.max(np.abs(x0), axis=(1,), keepdims=True) / 448.0).astype(np.float32)
    out = {}
    for k, v in d.items():
        if k == 'x':
            out['x_bytes'] = e4m3fn_bytes(x0 / s.astype(np.float64))
            out['x_scale'] = s
        else:
            out[k] = v
    return out


def reference(r, w2t, d, x_bytes, x_scale, w1t_words, w1t_scales, v, lam):
    return core(r, w2t, d, e4m3fn_values(x_bytes) * x_scale.astype(np.float64), w1t_words, w1t_scales, v, lam)

@@ -1,0 +1,501 @@
+from contextlib import ExitStack
+
+import concourse.mybir as mybir
+from concourse.masks import make_identity
+
+M, C, F, I = 1024, 512, 1536, 1024
+FLOPS = 2 * M * C * F + 2 * M * F * I + 2 * I * M * F
+
+F32 = mybir.dt.float32
+BF16 = mybir.dt.bfloat16
+I32 = mybir.dt.int32
+U32 = mybir.dt.uint32
+U8 = mybir.dt.uint8
+FP8 = mybir.dt.float8_e4m3fn
+FP8X4 = mybir.dt.float8_e4m3fn_x4
+FP4X4 = mybir.dt.float4_e2m1fn_x4
+MULT = mybir.AluOpType.mult
+ADD = mybir.AluOpType.add
+COPY = mybir.ActivationFunctionType.Copy
+
+P = 128
+
+
+def tile_gauss_newton_pullback_s8_kernel(tc, r, w2t, d, x_bytes, x_scale, w1t_words, w1t_scales, v, lam, out_0, out_1):
+    nc = tc.nc
+    with ExitStack() as ctx:
+        keep = ctx.enter_context(tc.tile_pool(name="keep", bufs=1))
+        work = ctx.enter_context(tc.tile_pool(name="work", bufs=2))
+        psum = ctx.enter_context(tc.psum_pool(name="psum", bufs=2))
+
+        def kept(name, shape, dtype):
+            return keep.tile(shape, dtype, name=name, tag=name, bufs=1, align_bytes=64)
+
+        def rolling(name, shape, dtype, bufs):
+            return work.tile(shape, dtype, name=name, tag=name, bufs=bufs, align_bytes=64)
+
+        r_view = r.rearrange("(g p t) c -> g p t c", p=P, t=4)
+        w2_view = w2t.rearrange("(p t) f -> p t f", t=4)
+        d_view = d.rearrange("(g p t) f -> g p t f", p=P, t=4)
+        x_view = x_bytes.rearrange("(g p t) n -> g p (t n)", p=P, t=4)
+        v_view = v.rearrange("(a k p) f -> a p k f", p=P, k=4)
+
+        r_raw = [kept(f"r_raw{g}", [P, 4, 512], BF16) for g in range(2)]
+        w2_raw = [kept(f"w2_raw{h}", [P, 4, 512], BF16) for h in range(3)]
+        d_raw = [kept("d_raw00", [P, 4, 512], BF16), kept("d_raw01", [P, 4, 1024], BF16), kept("d_raw1", [P, 4, 1536], BF16)]
+        x_raw = [kept(f"x_raw{g}", [P, 4096], U8) for g in range(2)]
+        x_sc = kept("x_sc", [P, 2, 4], F32)
+        w1_words = kept("w1_words", [P, 3, 2048], U8)
+        w1_scales = kept("w1_scales", [P, 3, 1024], U8)
+        v_raw = [kept(f"v_raw{a}", [P, 4, 1536], BF16) for a in range(2)]
+        lam_raw = kept("lam_raw", [P, 8, 2], BF16)
+        lam32 = kept("lam32", [P, 8], F32)
+        ident = kept("ident", [P, P], F32)
+
+        make_identity(nc, ident[:])
+        nc.gpsimd.memset(w1_scales[:].rearrange("p g n -> p (g n)").bitcast(I32), 0)
+
+        def load(tile, source):
+            nc.sync.dma_start(out=tile, in_=source)
+
+        def w1_load():
+            load(w1_words[:].bitcast(I32), w1t_words.bitcast(I32).rearrange("g p n -> p g n"))
+            for quad in range(4):
+                load(w1_scales[32 * quad : 32 * quad + 4, :, :].bitcast(I32), w1t_scales.bitcast(I32).rearrange("g s n -> s g n")[4 * quad : 4 * quad + 4])
+
+        def lam_load():
+            with nc.allow_non_contiguous_dma(reason="one damping factor to a partition"):
+                nc.sync.dma_start(out=lam_raw[:, :, 0:1], in_=lam.rearrange("(k p o) -> p k o", p=P, o=1))
+
+        load(r_raw[0][:], r_view[0])
+        load(w2_raw[0][:], w2_view[:, :, 0:512])
+        load(w2_raw[1][:], w2_view[:, :, 512:1024])
+        load(d_raw[0][:], d_view[0][:, :, 0:512])
+        load(w2_raw[2][:], w2_view[:, :, 1024:1536])
+        load(d_raw[1][:], d_view[0][:, :, 512:1536])
+        load(r_raw[1][:], r_view[1])
+        load(x_sc[:], x_scale.rearrange("(g p t) o -> p g (t o)", p=P, t=4))
+        for g in range(2):
+            load(x_raw[g][:], x_view[g])
+        w1_load()
+        load(d_raw[2][:], d_view[1])
+        lam_load()
+        load(v_raw[0][:], v_view[0])
+        load(v_raw[1][:], v_view[1])
+
+
+        r_codes, r_scales = {}, {}
+        w2_codes, w2_scales = {}, {}
+        a_val, a_codes, a_scales = {}, {}, {}
+        t_val, t_codes, t_scales = {}, {}, {}
+        x_codes, x_scales = {}, {}
+
+        def quantize(name, value, width):
+            codes = kept(name + "_c", [P, width], U32)
+            scales = kept(name + "_s", [P, width], U8)
+            nc.vector.quantize_mx(out=codes[:].bitcast(FP8X4), scales=scales[:], in_=value)
+            return codes, scales
+
+        def d_block(g, h):
+            if g == 1:
+                return d_raw[2][:, :, 512 * h : 512 * (h + 1)]
+            return d_raw[0][:] if h == 0 else d_raw[1][:, :, 512 * (h - 1) : 512 * h]
+
+        rt, w2i, turned, banks, wide, grouped, xrows = {}, {}, {}, {}, {}, {}, {}
+
+        def r_turn(g, half):
+            bank = psum.tile([P, 4, P], F32, name="turned", tag="turned", bufs=2)
+            banks["r", g, half] = bank
+            for tt in range(2):
+                words = r_raw[g][:, 2 * half + tt, :].bitcast(F32)
+                for u in range(2):
+                    nc.tensor.transpose(bank[:, 2 * tt + u, :], words[:, u:256:2], ident[:])
+
+        def copier(engine):
+            return nc.scalar.copy if engine == "S" else nc.vector.tensor_copy
+
+        def r_copy(g, half, engine="S"):
+            if g not in rt:
+                rt[g] = rolling("rt", [P, 2048], BF16, 1)
+            copier(engine)(
+                out=rt[g][:].bitcast(F32)[:, 512 * half : 512 * (half + 1)].rearrange("q (t p u) -> q t p u", t=2, u=2),
+                in_=banks["r", g, half][:].rearrange("q (t u) p -> q t p u", u=2),
+            )
+
+        def r_quant(g):
+            r_codes[g], r_scales[g] = quantize(f"r{g}", rt[g][:], 512)
+
+        def w_group(h, engine="V", js=(0, 4)):
+            raw = w2_raw[h][:]
+            if h not in w2i:
+                w2i[h] = rolling("w2i", [P, 2048], BF16, 2)
+            copier(engine)(
+                out=w2i[h][:].rearrange("c (j q t) -> c j q t", j=4, t=4)[:, js[0]:js[1]],
+                in_=raw.rearrange("c t (q j) -> c j q t", j=4)[:, js[0]:js[1]],
+            )
+
+        def w_quant(h):
+            w2_codes[h], w2_scales[h] = quantize(f"w2{h}", w2i[h][:], 512)
+
+        def gh(n):
+            return n // 3, n % 3
+
+        def s1(n, j):
+            g, h = gh(n)
+            bank = psum.tile([P, 4, P], F32, name="s1", tag="s1", bufs=2)
+            banks["s1", n, j] = bank
+            for t in range(4):
+                nc.tensor.matmul_mx(
+                    out=bank[:, t, :],
+                    lhsT=r_codes[g][:, P * t : P * (t + 1)].bitcast(FP8X4),
+                    lhsT_scale=r_scales[g][:, P * t : P * (t + 1)],
+                    rhs=w2_codes[h][:, P * j : P * (j + 1)].bitcast(FP8X4),
+                    rhs_scale=w2_scales[h][:, P * j : P * (j + 1)],
+                    start=True,
+                    stop=True,
+                )
+
+        def m(n, j):
+            g, h = gh(n)
+            if n not in a_val:
+                a_val[n] = rolling("a_val", [P, 512, 4], BF16, 6)
+            nc.vector.tensor_tensor(
+                out=a_val[n][:, P * j : P * (j + 1), :],
+                in0=banks["s1", n, j][:].rearrange("p t q -> p q t"),
+                in1=d_block(g, h).rearrange("p t (q j) -> p j q t", j=4)[:, j],
+                op=MULT,
+            )
+
+        def turn(n, u, js=(0, 4)):
+            words = a_val[n][:].rearrange("p f t -> p (f t)").bitcast(F32)
+            if js[0] == 0:
+                banks["t", n, u] = psum.tile([P, 4, P], F32, name="turned", tag="turned", bufs=2)
+            for j in range(*js):
+                nc.tensor.transpose(banks["t", n, u][:, j, :], words[:, 256 * j + u : 256 * (j + 1) : 2], ident[:])
+
+        def t_copy(n, u, engine="S"):
+            if n not in turned:
+                turned[n] = rolling("t_val", [P, 2048], BF16, 2)
+            copier(engine)(
+                out=turned[n][:, 1024 * u : 1024 * (u + 1)].rearrange("q (e p j) -> q e p j", e=2, j=4),
+                in_=banks["t", n, u][:].bitcast(BF16).rearrange("q j (p e) -> q e p j", e=2),
+            )
+
+        def qt(n):
+            t_codes[n], t_scales[n] = quantize(f"t{n}", turned[n][:], 512)
+
+        def qa(n):
+            a_codes[n], a_scales[n] = quantize(f"a{n}", a_val[n][:].rearrange("p f t -> p (f t)"), 512)
+
+        def dx(g, t, ih, hs=(0, 3)):
+            if hs[0] == 0:
+                banks["dx", g, t, ih] = psum.tile([P, 512], F32, name="acc", tag="acc", bufs=4)
+            bank = banks["dx", g, t, ih]
+            for h in range(*hs):
+                nc.tensor.matmul_mx(
+                    out=bank[:],
+                    lhsT=t_codes[3 * g + h][:, P * t : P * (t + 1)].bitcast(FP8X4),
+                    lhsT_scale=t_scales[3 * g + h][:, P * t : P * (t + 1)],
+                    rhs=w1_words[:, h, 1024 * ih : 1024 * (ih + 1)].bitcast(FP4X4),
+                    rhs_scale=w1_scales[:, h, 512 * ih : 512 * (ih + 1)],
+                    start=h == 0,
+                    stop=h == 2,
+                )
+
+        def dx_out(g, t, ih, engine="S"):
+            first = False
+            if (g, t) not in xrows:
+                first = True
+                xrows[g, t] = rolling("dx_rows", [P, I], F32, 3)
+            copier(engine)(out=xrows[g, t][:, 512 * ih : 512 * (ih + 1)], in_=banks["dx", g, t, ih][:])
+            if not first:
+                nc.sync.dma_start(out=out_0.rearrange("(g p t) i -> g p t i", p=P, t=4)[g][:, t, :], in_=xrows[g, t][:])
+
+        def xw(g, ih, t):
+            if (g, ih) not in wide:
+                wide[g, ih] = rolling("x_wide", [P, 4, 512], BF16, 2)
+            nc.scalar.activation(
+                out=wide[g, ih][:, t, :],
+                in_=x_raw[g][:, 1024 * t + 512 * ih : 1024 * t + 512 * (ih + 1)].bitcast(FP8),
+                func=COPY,
+                scale=x_sc[:, g, t : t + 1],
+            )
+
+        def xi(g, ih, engine="V"):
+            grouped[g, ih] = rolling("x_grouped", [P, 512, 4], BF16, 2)
+            copier(engine)(out=grouped[g, ih][:], in_=wide[g, ih][:].rearrange("p t n -> p n t"))
+
+        def xq(g, ih):
+            x_codes[g, ih], x_scales[g, ih] = quantize(f"x{g}{ih}", grouped[g, ih][:].rearrange("p n t -> p (n t)"), 512)
+
+        def gv(k, h):
+            ih, cols = k // 4, slice(P * (k % 4), P * (k % 4 + 1))
+            bank = psum.tile([P, 512], F32, name="acc", tag="acc", bufs=4)
+            banks["gv", k, h] = bank
+            for g in range(2):
+                nc.tensor.matmul_mx(
+                    out=bank[:],
+                    lhsT=x_codes[g, ih][:, cols].bitcast(FP8X4),
+                    lhsT_scale=x_scales[g, ih][:, cols],
+                    rhs=a_codes[3 * g + h][:].bitcast(FP8X4),
+                    rhs_scale=a_scales[3 * g + h][:],
+                    start=g == 0,
+                    stop=g == 1,
+                )
+
+        def e(k, h):
+            block = rolling("gv_block", [P, 512], F32, 6)
+            nc.vector.scalar_tensor_tensor(
+                out=block[:].rearrange("i (q j) -> i q j", j=4),
+                in0=v_raw[k // 4][:, k % 4, 512 * h : 512 * (h + 1)].rearrange("i (q j) -> i q j", j=4),
+                scalar=lam32[:, k : k + 1],
+                in1=banks["gv", k, h][:].rearrange("i (j q) -> i q j", j=4),
+                op0=MULT,
+                op1=ADD,
+            )
+            nc.sync.dma_start(out=out_1[P * k : P * (k + 1), 512 * h : 512 * (h + 1)], in_=block[:])
+
+        def lam_cast():
+            nc.vector.tensor_copy(out=lam32[:], in_=lam_raw[:, :, 0])
+
+        with tc.manual_schedule():
+            r_turn(0,0)
+            r_turn(0,1)
+            r_copy(0,0, "S")
+            w_group(0, "V", (0, 2))
+            w_group(0, "V", (2, 4))
+            r_copy(0,1, "S")
+            w_group(1, "S", (0, 2))
+            r_quant(0)
+            w_quant(0)
+            w_group(1, "V", (2, 4))
+            s1(0,0)
+            s1(0,1)
+            m(0,0)
+            w_group(2, "S", (0, 2))
+            w_quant(1)
+            s1(0,2)
+            m(0,1)
+            w_group(2, "S", (2, 4))
+            m(0,2)
+            s1(0,3)
+            m(0,3)
+            s1(1,0)
+            m(1,0)
+            s1(1,1)
+            turn(0,0)
+            w_quant(2)
+            turn(0,1)
+            t_copy(0,0, "S")
+            m(1,1)
+            s1(1,2)
+            qa(0)
+            s1(1,3)
+            t_copy(0,1, "S")
+            m(1,2)
+            r_turn(1,0)
+            m(1,3)
+            s1(2,0)
+            r_copy(1,0, "S")
+            qt(0)
+            r_turn(1,1)
+            xw(0,0,0)
+            m(2,0)
+            turn(1,0)
+            r_copy(1,1, "S")
+            qa(1)
+            s1(2,1)
+            t_copy(1,0, "S")
+            s1(2,2)
+            r_quant(1)
+            turn(1,1)
+            m(2,1)
+            t_copy(1,1, "S")
+            dx(0,0,0, (0, 1))
+            m(2,2)
+            s1(2,3)
+            dx(0,0,1, (0, 1))
+            m(2,3)
+            s1(3,0)
+            xw(0,0,1)
+            dx(0,1,0, (0, 1))
+            qt(1)
+            turn(2,0)
+            xw(0,0,2)
+            m(3,0)
+            xw(0,0,3)
+            dx(0,0,0, (1, 2))
+            qa(2)
+            turn(2,1)
+            t_copy(2,0, "S")
+            xi(0,0, "V")
+            dx(0,0,1, (1, 2))
+            s1(3,1)
+            t_copy(2,1, "S")
+            dx(0,1,0, (1, 2))
+            s1(3,2)
+            dx(0,1,1, (0, 1))
+            m(3,1)
+            dx(0,1,1, (1, 2))
+            xw(1,0,0)
+            m(3,2)
+            s1(3,3)
+            xw(1,0,1)
+            qt(2)
+            s1(4,0)
+            xw(1,0,2)
+            m(3,3)
+            dx(0,0,0, (2, 3))
+            dx(0,0,1, (2, 3))
+            dx_out(0,0,0, "S")
+            xq(0,0)
+            dx(0,1,0, (2, 3))
+            dx(0,1,1, (2, 3))
+            dx_out(0,0,1, "S")
+            m(4,0)
+            dx(0,2,0, (0, 1))
+            dx(0,2,0, (1, 2))
+            dx_out(0,1,0, "S")
+            qa(3)
+            dx(0,2,0, (2, 3))
+            dx(0,2,1, (0, 1))
+            xw(1,0,3)
+            dx(0,2,1, (1, 2))
+            dx(0,2,1, (2, 3))
+            dx_out(0,1,1, "S")
+            xi(1,0, "V")
+            turn(3,0)
+            dx_out(0,2,0, "S")
+            turn(3,1)
+            dx_out(0,2,1, "S")
+            dx(0,3,0, (0, 1))
+            t_copy(3,0, "S")
+            xq(1,0)
+            dx(0,3,0, (1, 2))
+            dx(0,3,0, (2, 3))
+            s1(4,1)
+            dx(0,3,1, (0, 1))
+            m(4,1)
+            t_copy(3,1, "S")
+            dx(0,3,1, (1, 2))
+            dx(0,3,1, (2, 3))
+            s1(4,2)
+            s1(4,3)
+            dx_out(0,3,0, "S")
+            m(4,2)
+            gv(0,0)
+            dx_out(0,3,1, "S")
+            qt(3)
+            s1(5,0)
+            xw(0,1,0)
+            gv(1,0)
+            m(4,3)
+            xw(0,1,1)
+            m(5,0)
+            s1(5,1)
+            xw(0,1,2)
+            turn(4,0)
+            m(5,1)
+            turn(4,1)
+            t_copy(4,0, "S")
+            lam_cast()
+            e(0,0)
+            e(1,0)
+            s1(5,2)
+            s1(5,3)
+            t_copy(4,1, "S")
+            m(5,2)
+            gv(2,0)
+            m(5,3)
+            gv(3,0)
+            xw(0,1,3)
+            qt(4)
+            turn(5,0)
+            xw(1,1,0)
+            e(2,0)
+            turn(5,1)
+            t_copy(5,0, "S")
+            qa(4)
+            dx(1,0,0, (0, 1))
+            dx(1,0,0, (1, 2))
+            e(3,0)
+            gv(0,1)
+            t_copy(5,1, "S")
+            qa(5)
+            gv(1,1)
+            e(0,1)
+            gv(0,2)
+            xw(1,1,1)
+            e(1,1)
+            gv(1,2)
+            xw(1,1,2)
+            e(0,2)
+            gv(2,1)
+            xw(1,1,3)
+            e(1,2)
+            gv(2,2)
+            xi(0,1, "S")
+            qt(5)
+            gv(3,1)
+            e(2,1)
+            dx(1,0,0, (2, 3))
+            e(2,2)
+            gv(3,2)
+            xi(1,1, "V")
+            dx(1,0,1, (0, 1))
+            dx(1,0,1, (1, 2))
+            dx_out(1,0,0, "S")
+            dx(1,0,1, (2, 3))
+            dx_out(1,0,1, "S")
+            dx(1,1,0, (0, 1))
+            xq(0,1)
+            dx(1,1,0, (1, 2))
+            dx(1,1,0, (2, 3))
+            xq(1,1)
+            dx(1,1,1, (0, 1))
+            dx_out(1,1,0, "S")
+            dx(1,1,1, (1, 2))
+            e(3,1)
+            dx(1,1,1, (2, 3))
+            gv(4,0)
+            dx_out(1,1,1, "S")
+            e(3,2)
+            gv(4,1)
+            e(4,0)
+            gv(4,2)
+            e(4,1)
+            dx(1,2,0, (0, 1))
+            e(4,2)
+            dx(1,2,0, (1, 2))
+            dx(1,2,0, (2, 3))
+            dx(1,2,1, (0, 1))
+            dx_out(1,2,0, "S")
+            dx(1,2,1, (1, 2))
+            dx(1,2,1, (2, 3))
+            gv(5,0)
+            dx_out(1,2,1, "S")
+            gv(5,1)
+            e(5,0)
+            dx(1,3,0, (0, 1))
+            e(5,1)
+            dx(1,3,0, (1, 2))
+            dx(1,3,0, (2, 3))
+            gv(5,2)
+            dx_out(1,3,0, "S")
+            dx(1,3,1, (0, 1))
+            e(5,2)
+            dx(1,3,1, (1, 2))
+            dx(1,3,1, (2, 3))
+            gv(6,0)
+            dx_out(1,3,1, "S")
+            gv(6,1)
+            e(6,0)
+            gv(6,2)
+            e(6,1)
+            gv(7,0)
+            e(6,2)
+            gv(7,1)
+            e(7,0)
+            gv(7,2)
+            e(7,1)
+            e(7,2)

@@ -38,57 +38,62 @@ def tile_gauss_newton_pullback_s8_kernel(tc, r, w2t, d, x_bytes, x_scale, w1t_wo
         w2_view = w2t.rearrange("(p t) f -> p t f", t=4)
         d_view = d.rearrange("(g p t) f -> g p t f", p=P, t=4)
         x_view = x_bytes.rearrange("(g p t) n -> g p (t n)", p=P, t=4)
-        v_view = v.rearrange("(a k p) f -> a p k f", p=P, k=4)
+        v_view = v.rearrange("(a k p) f -> a p k f", p=P, k=2)
+        dx_view = out_0.rearrange("(g p t) i -> g p t i", p=P, t=4)
 
-        r_raw = [kept(f"r_raw{g}", [P, 4, 512], BF16) for g in range(2)]
+        r_raw = [kept("r_raw0", [P, 2, 512], BF16), kept("r_raw1", [P, 2, 512], BF16), kept("r_raw23", [P, 4, 512], BF16)]
         w2_raw = [kept(f"w2_raw{h}", [P, 4, 512], BF16) for h in range(3)]
-        d_raw = [kept("d_raw00", [P, 4, 512], BF16), kept("d_raw01", [P, 4, 1024], BF16), kept("d_raw1", [P, 4, 1536], BF16)]
+        d00 = kept("d00", [P, 2, 512], BF16)
+        d01 = kept("d01", [P, 2, 1024], BF16)
+        d1, d2, d3 = [rolling("six", [P, 2, 1536], BF16, 5) for _ in range(3)]
+        v_raw = {}
         x_raw = [kept(f"x_raw{g}", [P, 4096], U8) for g in range(2)]
         x_sc = kept("x_sc", [P, 2, 4], F32)
         w1_words = kept("w1_words", [P, 3, 2048], U8)
         w1_scales = kept("w1_scales", [P, 3, 1024], U8)
-        v_raw = [kept(f"v_raw{a}", [P, 4, 1536], BF16) for a in range(2)]
-        lam_raw = kept("lam_raw", [P, 8, 2], BF16)
+        lam_rows = kept("lam_rows", [P, P], BF16)
         lam32 = kept("lam32", [P, 8], F32)
         ident = kept("ident", [P, P], F32)
+        ident16 = kept("ident16", [P, P], BF16)
 
         make_identity(nc, ident[:])
+        nc.gpsimd.memset(lam_rows[:], 0)
         nc.gpsimd.memset(w1_scales[:].rearrange("p g n -> p (g n)").bitcast(I32), 0)
 
         def load(tile, source):
             nc.sync.dma_start(out=tile, in_=source)
 
-        def w1_load():
-            load(w1_words[:].bitcast(I32), w1t_words.bitcast(I32).rearrange("g p n -> p g n"))
+        def load_v(a):
+            v_raw[a] = rolling("six", [P, 2, 1536], BF16, 5)
+            load(v_raw[a][:], v_view[a])
+
+        def w1_scale_load():
             for quad in range(4):
                 load(w1_scales[32 * quad : 32 * quad + 4, :, :].bitcast(I32), w1t_scales.bitcast(I32).rearrange("g s n -> s g n")[4 * quad : 4 * quad + 4])
 
-        def lam_load():
-            with nc.allow_non_contiguous_dma(reason="one damping factor to a partition"):
-                nc.sync.dma_start(out=lam_raw[:, :, 0:1], in_=lam.rearrange("(k p o) -> p k o", p=P, o=1))
-
-        load(r_raw[0][:], r_view[0])
         load(w2_raw[0][:], w2_view[:, :, 0:512])
+        load(r_raw[0][:], r_view[0][:, 0:2, :])
+        load(d00[:], d_view[0][:, 0:2, 0:512])
         load(w2_raw[1][:], w2_view[:, :, 512:1024])
-        load(d_raw[0][:], d_view[0][:, :, 0:512])
+        load(d01[:], d_view[0][:, 0:2, 512:1536])
         load(w2_raw[2][:], w2_view[:, :, 1024:1536])
-        load(d_raw[1][:], d_view[0][:, :, 512:1536])
-        load(r_raw[1][:], r_view[1])
+        load(r_raw[1][:], r_view[0][:, 2:4, :])
+        load(d1[:], d_view[0][:, 2:4, :])
+        load(w1_words[:].bitcast(I32), w1t_words.bitcast(I32).rearrange("g p n -> p g n"))
+        w1_scale_load()
         load(x_sc[:], x_scale.rearrange("(g p t) o -> p g (t o)", p=P, t=4))
         for g in range(2):
             load(x_raw[g][:], x_view[g])
-        w1_load()
-        load(d_raw[2][:], d_view[1])
-        lam_load()
-        load(v_raw[0][:], v_view[0])
-        load(v_raw[1][:], v_view[1])
+        load(r_raw[2][:], r_view[1])
+        load(lam_rows[0:8, :], lam.rearrange("(k p) -> k p", p=P))
+        load(d2[:], d_view[1][:, 0:2, :])
+        load(d3[:], d_view[1][:, 2:4, :])
+        load_v(0)
+        load_v(1)
 
-
-        r_codes, r_scales = {}, {}
-        w2_codes, w2_scales = {}, {}
-        a_val, a_codes, a_scales = {}, {}, {}
-        t_val, t_codes, t_scales = {}, {}, {}
-        x_codes, x_scales = {}, {}
+        r_codes, r_scales, w2_codes, w2_scales = {}, {}, {}, {}
+        a_codes, a_scales, t_codes, t_scales, x_codes, x_scales = {}, {}, {}, {}, {}, {}
+        rt_val, w2i, b_val, a_val, t_val, wide, grouped, banks, blocks = {}, {}, {}, {}, {}, {}, {}, {}, {}
 
         def quantize(name, value, width):
             codes = kept(name + "_c", [P, width], U32)
@@ -96,406 +101,431 @@ def tile_gauss_newton_pullback_s8_kernel(tc, r, w2t, d, x_bytes, x_scale, w1t_wo
             nc.vector.quantize_mx(out=codes[:].bitcast(FP8X4), scales=scales[:], in_=value)
             return codes, scales
 
-        def d_block(g, h):
-            if g == 1:
-                return d_raw[2][:, :, 512 * h : 512 * (h + 1)]
-            return d_raw[0][:] if h == 0 else d_raw[1][:, :, 512 * (h - 1) : 512 * h]
-
-        rt, w2i, turned, banks, wide, grouped, xrows = {}, {}, {}, {}, {}, {}, {}
-
-        def r_turn(g, half):
-            bank = psum.tile([P, 4, P], F32, name="turned", tag="turned", bufs=2)
-            banks["r", g, half] = bank
-            for tt in range(2):
-                words = r_raw[g][:, 2 * half + tt, :].bitcast(F32)
-                for u in range(2):
-                    nc.tensor.transpose(bank[:, 2 * tt + u, :], words[:, u:256:2], ident[:])
-
         def copier(engine):
             return nc.scalar.copy if engine == "S" else nc.vector.tensor_copy
 
-        def r_copy(g, half, engine="S"):
-            if g not in rt:
-                rt[g] = rolling("rt", [P, 2048], BF16, 1)
+        def spread(engine, out, in_):
+            if engine == "G":
+                nc.gpsimd.tensor_scalar(out=out, in0=in_, scalar1=1.0, scalar2=0.0, op0=MULT, op1=ADD)
+            else:
+                copier(engine)(out=out, in_=in_)
+
+        def lam_ident():
+            nc.vector.tensor_copy(out=ident16[:], in_=ident[:])
+
+        def lam_turn():
+            bank = banks["lam"] = psum.tile([P, P], BF16, name="turned", tag="turned", bufs=2)
+            nc.tensor.transpose(bank[:], lam_rows[:], ident16[:])
+
+        def lam_copy():
+            nc.vector.tensor_copy(out=lam32[:], in_=banks["lam"][:, 0:8])
+
+        def rt(s):
+            banks["r", s] = psum.tile([P, 4, P], F32, name="turned", tag="turned", bufs=2)
+            for e in range(2):
+                raw = r_raw[s][:, e, :] if s < 2 else r_raw[2][:, 2 * (s - 2) + e, :]
+                for u in range(2):
+                    nc.tensor.transpose(banks["r", s][:, 2 * e + u, :], raw.bitcast(F32)[:, u:256:2], ident[:])
+
+        def rc(s, engine):
+            rt_val[s] = rolling("rt_val", [P, 1024], BF16, 2)
             copier(engine)(
-                out=rt[g][:].bitcast(F32)[:, 512 * half : 512 * (half + 1)].rearrange("q (t p u) -> q t p u", t=2, u=2),
-                in_=banks["r", g, half][:].rearrange("q (t u) p -> q t p u", u=2),
+                out=rt_val[s][:].bitcast(F32).rearrange("q (e p u) -> q e p u", e=2, u=2),
+                in_=banks["r", s][:].rearrange("q (e u) p -> q e p u", u=2),
             )
 
-        def r_quant(g):
-            r_codes[g], r_scales[g] = quantize(f"r{g}", rt[g][:], 512)
+        def rq(s):
+            r_codes[s], r_scales[s] = quantize(f"r{s}", rt_val[s][:], 256)
 
-        def w_group(h, engine="V", js=(0, 4)):
-            raw = w2_raw[h][:]
+        def wg(h, f, engine):
             if h not in w2i:
-                w2i[h] = rolling("w2i", [P, 2048], BF16, 2)
-            copier(engine)(
-                out=w2i[h][:].rearrange("c (j q t) -> c j q t", j=4, t=4)[:, js[0]:js[1]],
-                in_=raw.rearrange("c t (q j) -> c j q t", j=4)[:, js[0]:js[1]],
+                w2i[h] = rolling("w2i", [P, 512, 4], BF16, 2)
+            cols = slice(256 * f, 256 * (f + 1))
+            spread(engine, w2i[h][:, cols, :], w2_raw[h][:, :, cols].rearrange("c t f -> c f t"))
+
+        def wq(h):
+            w2_codes[h], w2_scales[h] = quantize(f"w2{h}", w2i[h][:].rearrange("c f t -> c (f t)"), 512)
+
+        def s1(s, h, e):
+            banks["s1", s, h, e] = psum.tile([P, 512], F32, name="s1", tag="s1", bufs=3)
+            cols = slice(P * e, P * (e + 1))
+            nc.tensor.matmul_mx(
+                out=banks["s1", s, h, e][:],
+                lhsT=r_codes[s][:, cols].bitcast(FP8X4),
+                lhsT_scale=r_scales[s][:, cols],
+                rhs=w2_codes[h][:].bitcast(FP8X4),
+                rhs_scale=w2_scales[h][:],
+                start=True,
+                stop=True,
             )
 
-        def w_quant(h):
-            w2_codes[h], w2_scales[h] = quantize(f"w2{h}", w2i[h][:], 512)
+        def d_row(s, h, e):
+            if s == 0:
+                return d00[:, e, :] if h == 0 else d01[:, e, 512 * (h - 1) : 512 * h]
+            if s == 1:
+                return d1[:, e, 512 * h : 512 * (h + 1)]
+            return (d2 if s == 2 else d3)[:, e, 512 * h : 512 * (h + 1)]
 
-        def gh(n):
-            return n // 3, n % 3
-
-        def s1(n, j):
-            g, h = gh(n)
-            bank = psum.tile([P, 4, P], F32, name="s1", tag="s1", bufs=2)
-            banks["s1", n, j] = bank
-            for t in range(4):
-                nc.tensor.matmul_mx(
-                    out=bank[:, t, :],
-                    lhsT=r_codes[g][:, P * t : P * (t + 1)].bitcast(FP8X4),
-                    lhsT_scale=r_scales[g][:, P * t : P * (t + 1)],
-                    rhs=w2_codes[h][:, P * j : P * (j + 1)].bitcast(FP8X4),
-                    rhs_scale=w2_scales[h][:, P * j : P * (j + 1)],
-                    start=True,
-                    stop=True,
-                )
-
-        def m(n, j):
-            g, h = gh(n)
-            if n not in a_val:
-                a_val[n] = rolling("a_val", [P, 512, 4], BF16, 6)
+        def m(s, h, e):
+            g = s // 2
+            if (g, h) not in b_val:
+                b_val[g, h] = rolling("b_val", [P, 4, 512], BF16, 6)
             nc.vector.tensor_tensor(
-                out=a_val[n][:, P * j : P * (j + 1), :],
-                in0=banks["s1", n, j][:].rearrange("p t q -> p q t"),
-                in1=d_block(g, h).rearrange("p t (q j) -> p j q t", j=4)[:, j],
+                out=b_val[g, h][:, 2 * (s % 2) + e, :].rearrange("p (u q i) -> p u q i", u=2, i=2),
+                in0=banks["s1", s, h, e][:].rearrange("p (q u i) -> p u q i", u=2, i=2),
+                in1=d_row(s, h, e).rearrange("p (q u i) -> p u q i", u=2, i=2),
                 op=MULT,
             )
 
-        def turn(n, u, js=(0, 4)):
-            words = a_val[n][:].rearrange("p f t -> p (f t)").bitcast(F32)
-            if js[0] == 0:
-                banks["t", n, u] = psum.tile([P, 4, P], F32, name="turned", tag="turned", bufs=2)
-            for j in range(*js):
-                nc.tensor.transpose(banks["t", n, u][:, j, :], words[:, 256 * j + u : 256 * (j + 1) : 2], ident[:])
+        def tn(s, h):
+            banks["t", s, h] = psum.tile([P, 4, P], F32, name="turned", tag="turned", bufs=2)
+            for e in range(2):
+                words = b_val[s // 2, h][:, 2 * (s % 2) + e, :].bitcast(F32)
+                for u in range(2):
+                    nc.tensor.transpose(banks["t", s, h][:, 2 * e + u, :], words[:, P * u : P * (u + 1)], ident[:])
 
-        def t_copy(n, u, engine="S"):
-            if n not in turned:
-                turned[n] = rolling("t_val", [P, 2048], BF16, 2)
+        def tc_(s, h, engine):
+            t_val[s, h] = rolling("t_val", [P, 1024], BF16, 4)
             copier(engine)(
-                out=turned[n][:, 1024 * u : 1024 * (u + 1)].rearrange("q (e p j) -> q e p j", e=2, j=4),
-                in_=banks["t", n, u][:].bitcast(BF16).rearrange("q j (p e) -> q e p j", e=2),
+                out=t_val[s, h][:].bitcast(F32).rearrange("q (e p u) -> q e p u", e=2, u=2),
+                in_=banks["t", s, h][:].rearrange("q (e u) p -> q e p u", u=2),
             )
 
-        def qt(n):
-            t_codes[n], t_scales[n] = quantize(f"t{n}", turned[n][:], 512)
+        def qt(s, h):
+            t_codes[s, h], t_scales[s, h] = quantize(f"t{s}{h}", t_val[s, h][:], 256)
 
-        def qa(n):
-            a_codes[n], a_scales[n] = quantize(f"a{n}", a_val[n][:].rearrange("p f t -> p (f t)"), 512)
-
-        def dx(g, t, ih, hs=(0, 3)):
-            if hs[0] == 0:
-                banks["dx", g, t, ih] = psum.tile([P, 512], F32, name="acc", tag="acc", bufs=4)
-            bank = banks["dx", g, t, ih]
-            for h in range(*hs):
+        def dx(s, e, ih):
+            bank = psum.tile([P, 512], F32, name="acc", tag="acc", bufs=3)
+            banks["dx", s, e, ih] = bank
+            for h in range(3):
                 nc.tensor.matmul_mx(
                     out=bank[:],
-                    lhsT=t_codes[3 * g + h][:, P * t : P * (t + 1)].bitcast(FP8X4),
-                    lhsT_scale=t_scales[3 * g + h][:, P * t : P * (t + 1)],
+                    lhsT=t_codes[s, h][:, P * e : P * (e + 1)].bitcast(FP8X4),
+                    lhsT_scale=t_scales[s, h][:, P * e : P * (e + 1)],
                     rhs=w1_words[:, h, 1024 * ih : 1024 * (ih + 1)].bitcast(FP4X4),
                     rhs_scale=w1_scales[:, h, 512 * ih : 512 * (ih + 1)],
                     start=h == 0,
                     stop=h == 2,
                 )
 
-        def dx_out(g, t, ih, engine="S"):
-            first = False
-            if (g, t) not in xrows:
-                first = True
-                xrows[g, t] = rolling("dx_rows", [P, I], F32, 3)
-            copier(engine)(out=xrows[g, t][:, 512 * ih : 512 * (ih + 1)], in_=banks["dx", g, t, ih][:])
-            if not first:
-                nc.sync.dma_start(out=out_0.rearrange("(g p t) i -> g p t i", p=P, t=4)[g][:, t, :], in_=xrows[g, t][:])
+        def do(s, e, ih, engine):
+            block = rolling("block", [P, 512], F32, 13)
+            copier(engine)(out=block[:], in_=banks["dx", s, e, ih][:])
+            nc.sync.dma_start(out=dx_view[s // 2][:, 2 * (s % 2) + e, 512 * ih : 512 * (ih + 1)], in_=block[:])
 
-        def xw(g, ih, t):
+        def ai(g, h, u, engine):
+            if (g, h) not in a_val:
+                a_val[g, h] = rolling("a_val", [P, 512, 4], BF16, 4)
+            spread(
+                engine,
+                a_val[g, h][:].rearrange("p (q u i) t -> p u q i t", u=2, i=2)[:, u],
+                b_val[g, h][:].rearrange("p t (u q i) -> p u q i t", u=2, i=2)[:, u],
+            )
+
+        def qa(g, h):
+            a_codes[g, h], a_scales[g, h] = quantize(f"a{g}{h}", a_val[g, h][:].rearrange("p f t -> p (f t)"), 512)
+
+        def xw(g, ih, t, engine):
             if (g, ih) not in wide:
-                wide[g, ih] = rolling("x_wide", [P, 4, 512], BF16, 2)
+                wide[g, ih] = rolling("x_wide", [P, 4, 512], BF16, 4)
             nc.scalar.activation(
                 out=wide[g, ih][:, t, :],
                 in_=x_raw[g][:, 1024 * t + 512 * ih : 1024 * t + 512 * (ih + 1)].bitcast(FP8),
                 func=COPY,
                 scale=x_sc[:, g, t : t + 1],
+            ) if engine == "S" else nc.vector.tensor_scalar(
+                out=wide[g, ih][:, t, :],
+                in0=x_raw[g][:, 1024 * t + 512 * ih : 1024 * t + 512 * (ih + 1)].bitcast(FP8),
+                scalar1=x_sc[:, g, t : t + 1],
+                scalar2=None,
+                op0=MULT,
             )
 
-        def xi(g, ih, engine="V"):
-            grouped[g, ih] = rolling("x_grouped", [P, 512, 4], BF16, 2)
-            copier(engine)(out=grouped[g, ih][:], in_=wide[g, ih][:].rearrange("p t n -> p n t"))
+        def xi(g, ih, f, engine):
+            if (g, ih) not in grouped:
+                grouped[g, ih] = rolling("x_grouped", [P, 512, 4], BF16, 2)
+            cols = slice(256 * f, 256 * (f + 1))
+            spread(engine, grouped[g, ih][:, cols, :], wide[g, ih][:, :, cols].rearrange("p t n -> p n t"))
 
         def xq(g, ih):
             x_codes[g, ih], x_scales[g, ih] = quantize(f"x{g}{ih}", grouped[g, ih][:].rearrange("p n t -> p (n t)"), 512)
 
         def gv(k, h):
             ih, cols = k // 4, slice(P * (k % 4), P * (k % 4 + 1))
-            bank = psum.tile([P, 512], F32, name="acc", tag="acc", bufs=4)
+            bank = psum.tile([P, 512], F32, name="acc", tag="acc", bufs=3)
             banks["gv", k, h] = bank
             for g in range(2):
                 nc.tensor.matmul_mx(
                     out=bank[:],
                     lhsT=x_codes[g, ih][:, cols].bitcast(FP8X4),
                     lhsT_scale=x_scales[g, ih][:, cols],
-                    rhs=a_codes[3 * g + h][:].bitcast(FP8X4),
-                    rhs_scale=a_scales[3 * g + h][:],
+                    rhs=a_codes[g, h][:].bitcast(FP8X4),
+                    rhs_scale=a_scales[g, h][:],
                     start=g == 0,
                     stop=g == 1,
                 )
 
-        def e(k, h):
-            block = rolling("gv_block", [P, 512], F32, 6)
+        def ev(k, h):
+            block = rolling("block", [P, 512], F32, 13)
             nc.vector.scalar_tensor_tensor(
-                out=block[:].rearrange("i (q j) -> i q j", j=4),
-                in0=v_raw[k // 4][:, k % 4, 512 * h : 512 * (h + 1)].rearrange("i (q j) -> i q j", j=4),
+                out=block[:],
+                in0=v_raw[k // 2][:, k % 2, 512 * h : 512 * (h + 1)],
                 scalar=lam32[:, k : k + 1],
-                in1=banks["gv", k, h][:].rearrange("i (j q) -> i q j", j=4),
+                in1=banks["gv", k, h][:],
                 op0=MULT,
                 op1=ADD,
             )
             nc.sync.dma_start(out=out_1[P * k : P * (k + 1), 512 * h : 512 * (h + 1)], in_=block[:])
 
-        def lam_cast():
-            nc.vector.tensor_copy(out=lam32[:], in_=lam_raw[:, :, 0])
+        def lv(k, h):
+            blocks["l", k, h] = rolling("lam_v", [P, 512], F32, 3)
+            nc.scalar.activation(
+                out=blocks["l", k, h][:], in_=v_raw[k // 2][:, k % 2, 512 * h : 512 * (h + 1)], func=COPY, scale=lam32[:, k : k + 1]
+            )
+
+        def ec(k, h):
+            blocks["c", k, h] = rolling("gv_copy", [P, 512], F32, 3)
+            nc.scalar.copy(out=blocks["c", k, h][:], in_=banks["gv", k, h][:])
+
+        def eg(k, h):
+            block = rolling("block", [P, 512], F32, 13)
+            nc.gpsimd.tensor_tensor(out=block[:], in0=blocks["c", k, h][:], in1=blocks["l", k, h][:], op=ADD)
+            nc.sync.dma_start(out=out_1[P * k : P * (k + 1), 512 * h : 512 * (h + 1)], in_=block[:])
 
         with tc.manual_schedule():
-            r_turn(0,0)
-            r_turn(0,1)
-            r_copy(0,0, "S")
-            w_group(0, "V", (0, 2))
-            w_group(0, "V", (2, 4))
-            r_copy(0,1, "S")
-            w_group(1, "S", (0, 2))
-            r_quant(0)
-            w_quant(0)
-            w_group(1, "V", (2, 4))
-            s1(0,0)
-            s1(0,1)
-            m(0,0)
-            w_group(2, "S", (0, 2))
-            w_quant(1)
-            s1(0,2)
-            m(0,1)
-            w_group(2, "S", (2, 4))
-            m(0,2)
-            s1(0,3)
-            m(0,3)
-            s1(1,0)
-            m(1,0)
-            s1(1,1)
-            turn(0,0)
-            w_quant(2)
-            turn(0,1)
-            t_copy(0,0, "S")
-            m(1,1)
-            s1(1,2)
-            qa(0)
-            s1(1,3)
-            t_copy(0,1, "S")
-            m(1,2)
-            r_turn(1,0)
-            m(1,3)
-            s1(2,0)
-            r_copy(1,0, "S")
-            qt(0)
-            r_turn(1,1)
-            xw(0,0,0)
-            m(2,0)
-            turn(1,0)
-            r_copy(1,1, "S")
-            qa(1)
-            s1(2,1)
-            t_copy(1,0, "S")
-            s1(2,2)
-            r_quant(1)
-            turn(1,1)
-            m(2,1)
-            t_copy(1,1, "S")
-            dx(0,0,0, (0, 1))
-            m(2,2)
-            s1(2,3)
-            dx(0,0,1, (0, 1))
-            m(2,3)
-            s1(3,0)
-            xw(0,0,1)
-            dx(0,1,0, (0, 1))
-            qt(1)
-            turn(2,0)
-            xw(0,0,2)
-            m(3,0)
-            xw(0,0,3)
-            dx(0,0,0, (1, 2))
-            qa(2)
-            turn(2,1)
-            t_copy(2,0, "S")
-            xi(0,0, "V")
-            dx(0,0,1, (1, 2))
-            s1(3,1)
-            t_copy(2,1, "S")
-            dx(0,1,0, (1, 2))
-            s1(3,2)
-            dx(0,1,1, (0, 1))
-            m(3,1)
-            dx(0,1,1, (1, 2))
-            xw(1,0,0)
-            m(3,2)
-            s1(3,3)
-            xw(1,0,1)
-            qt(2)
-            s1(4,0)
-            xw(1,0,2)
-            m(3,3)
-            dx(0,0,0, (2, 3))
-            dx(0,0,1, (2, 3))
-            dx_out(0,0,0, "S")
-            xq(0,0)
-            dx(0,1,0, (2, 3))
-            dx(0,1,1, (2, 3))
-            dx_out(0,0,1, "S")
-            m(4,0)
-            dx(0,2,0, (0, 1))
-            dx(0,2,0, (1, 2))
-            dx_out(0,1,0, "S")
-            qa(3)
-            dx(0,2,0, (2, 3))
-            dx(0,2,1, (0, 1))
-            xw(1,0,3)
-            dx(0,2,1, (1, 2))
-            dx(0,2,1, (2, 3))
-            dx_out(0,1,1, "S")
-            xi(1,0, "V")
-            turn(3,0)
-            dx_out(0,2,0, "S")
-            turn(3,1)
-            dx_out(0,2,1, "S")
-            dx(0,3,0, (0, 1))
-            t_copy(3,0, "S")
-            xq(1,0)
-            dx(0,3,0, (1, 2))
-            dx(0,3,0, (2, 3))
-            s1(4,1)
-            dx(0,3,1, (0, 1))
-            m(4,1)
-            t_copy(3,1, "S")
-            dx(0,3,1, (1, 2))
-            dx(0,3,1, (2, 3))
-            s1(4,2)
-            s1(4,3)
-            dx_out(0,3,0, "S")
-            m(4,2)
-            gv(0,0)
-            dx_out(0,3,1, "S")
-            qt(3)
-            s1(5,0)
-            xw(0,1,0)
-            gv(1,0)
-            m(4,3)
-            xw(0,1,1)
-            m(5,0)
-            s1(5,1)
-            xw(0,1,2)
-            turn(4,0)
-            m(5,1)
-            turn(4,1)
-            t_copy(4,0, "S")
-            lam_cast()
-            e(0,0)
-            e(1,0)
-            s1(5,2)
-            s1(5,3)
-            t_copy(4,1, "S")
-            m(5,2)
-            gv(2,0)
-            m(5,3)
-            gv(3,0)
-            xw(0,1,3)
-            qt(4)
-            turn(5,0)
-            xw(1,1,0)
-            e(2,0)
-            turn(5,1)
-            t_copy(5,0, "S")
-            qa(4)
-            dx(1,0,0, (0, 1))
-            dx(1,0,0, (1, 2))
-            e(3,0)
-            gv(0,1)
-            t_copy(5,1, "S")
-            qa(5)
-            gv(1,1)
-            e(0,1)
-            gv(0,2)
-            xw(1,1,1)
-            e(1,1)
-            gv(1,2)
-            xw(1,1,2)
-            e(0,2)
-            gv(2,1)
-            xw(1,1,3)
-            e(1,2)
-            gv(2,2)
-            xi(0,1, "S")
-            qt(5)
-            gv(3,1)
-            e(2,1)
-            dx(1,0,0, (2, 3))
-            e(2,2)
-            gv(3,2)
-            xi(1,1, "V")
-            dx(1,0,1, (0, 1))
-            dx(1,0,1, (1, 2))
-            dx_out(1,0,0, "S")
-            dx(1,0,1, (2, 3))
-            dx_out(1,0,1, "S")
-            dx(1,1,0, (0, 1))
-            xq(0,1)
-            dx(1,1,0, (1, 2))
-            dx(1,1,0, (2, 3))
-            xq(1,1)
-            dx(1,1,1, (0, 1))
-            dx_out(1,1,0, "S")
-            dx(1,1,1, (1, 2))
-            e(3,1)
-            dx(1,1,1, (2, 3))
-            gv(4,0)
-            dx_out(1,1,1, "S")
-            e(3,2)
-            gv(4,1)
-            e(4,0)
-            gv(4,2)
-            e(4,1)
-            dx(1,2,0, (0, 1))
-            e(4,2)
-            dx(1,2,0, (1, 2))
-            dx(1,2,0, (2, 3))
-            dx(1,2,1, (0, 1))
-            dx_out(1,2,0, "S")
-            dx(1,2,1, (1, 2))
-            dx(1,2,1, (2, 3))
-            gv(5,0)
-            dx_out(1,2,1, "S")
-            gv(5,1)
-            e(5,0)
-            dx(1,3,0, (0, 1))
-            e(5,1)
-            dx(1,3,0, (1, 2))
-            dx(1,3,0, (2, 3))
-            gv(5,2)
-            dx_out(1,3,0, "S")
-            dx(1,3,1, (0, 1))
-            e(5,2)
-            dx(1,3,1, (1, 2))
-            dx(1,3,1, (2, 3))
-            gv(6,0)
-            dx_out(1,3,1, "S")
-            gv(6,1)
-            e(6,0)
-            gv(6,2)
-            e(6,1)
-            gv(7,0)
-            e(6,2)
-            gv(7,1)
-            e(7,0)
-            gv(7,2)
-            e(7,1)
-            e(7,2)
+            lam_ident()
+            wg(0, 0, "V")
+            wg(0, 1, "S")
+            rt(0)
+            wq(0)
+            rc(0, "V")
+            rq(0)
+            wg(1, 1, "S")
+            wg(1, 0, "V")
+            s1(0, 0, 0)
+            s1(0, 0, 1)
+            m(0, 0, 0)
+            wq(1)
+            m(0, 0, 1)
+            s1(0, 1, 0)
+            s1(0, 1, 1)
+            wg(2, 1, "S")
+            wg(2, 0, "V")
+            tn(0, 0)
+            rt(1)
+            m(0, 1, 0)
+            tc_(0, 0, "S")
+            wq(2)
+            rc(1, "S")
+            m(0, 1, 1)
+            s1(0, 2, 0)
+            s1(0, 2, 1)
+            rq(1)
+            tn(0, 1)
+            m(0, 2, 0)
+            tc_(0, 1, "S")
+            s1(1, 0, 0)
+            m(0, 2, 1)
+            s1(1, 1, 0)
+            m(1, 0, 0)
+            s1(1, 0, 1)
+            tn(0, 2)
+            m(1, 1, 0)
+            tc_(0, 2, "S")
+            s1(1, 2, 0)
+            m(1, 0, 1)
+            s1(1, 1, 1)
+            m(1, 2, 0)
+            s1(1, 2, 1)
+            ai(0, 0, 0, "S")
+            tn(1, 0)
+            m(1, 1, 1)
+            tc_(1, 0, "V")
+            tn(1, 1)
+            xw(0, 0, 3, "S")
+            qt(0, 0)
+            qt(1, 0)
+            tc_(1, 1, "S")
+            m(1, 2, 1)
+            load_v(2)
+            rt(2)
+            xw(1, 0, 3, "S")
+            qt(0, 1)
+            rt(3)
+            xw(0, 0, 2, "S")
+            rc(2, "V")
+            qt(1, 1)
+            rc(3, "S")
+            tn(1, 2)
+            rq(2)
+            xw(1, 0, 2, "S")
+            tc_(1, 2, "V")
+            lam_turn()
+            s1(2, 0, 0)
+            s1(2, 1, 0)
+            xw(0, 0, 1, "S")
+            rq(3)
+            s1(2, 0, 1)
+            lam_copy()
+            qt(0, 2)
+            xw(1, 0, 1, "S")
+            qt(1, 2)
+            dx(0, 0, 1)
+            m(2, 0, 0)
+            xw(0, 0, 0, "S")
+            m(2, 1, 0)
+            s1(2, 2, 0)
+            do(0, 0, 1, "S")
+            dx(0, 1, 1)
+            m(2, 0, 1)
+            xw(1, 0, 0, "S")
+            m(2, 2, 0)
+            s1(3, 0, 0)
+            xi(0, 0, 0, "S")
+            tn(2, 0)
+            do(0, 1, 1, "V")
+            s1(2, 1, 1)
+            xi(1, 0, 0, "V")
+            s1(3, 1, 0)
+            tc_(2, 0, "S")
+            dx(1, 0, 1)
+            xi(1, 0, 1, "V")
+            xi(0, 0, 1, "S")
+            dx(1, 1, 1)
+            m(3, 0, 0)
+            xq(1, 0)
+            s1(2, 2, 1)
+            do(1, 0, 1, "S")
+            dx(0, 0, 0)
+            xq(0, 0)
+            do(1, 1, 1, "S")
+            qt(2, 0)
+            dx(0, 1, 0)
+            do(0, 0, 0, "S")
+            m(2, 1, 1)
+            xw(0, 1, 3, "S")
+            do(0, 1, 0, "V")
+            s1(3, 0, 1)
+            xw(1, 1, 3, "S")
+            tn(2, 1)
+            m(3, 1, 0)
+            tc_(2, 1, "S")
+            dx(1, 0, 0)
+            m(2, 2, 1)
+            load_v(3)
+            xw(0, 1, 2, "S")
+            qt(2, 1)
+            s1(3, 2, 0)
+            do(1, 0, 0, "S")
+            m(3, 0, 1)
+            tn(2, 2)
+            tc_(2, 2, "S")
+            s1(3, 1, 1)
+            m(3, 2, 0)
+            tn(3, 0)
+            xw(1, 1, 2, "S")
+            qt(2, 2)
+            s1(3, 2, 1)
+            m(3, 1, 1)
+            tc_(3, 0, "S")
+            dx(2, 0, 1)
+            m(3, 2, 1)
+            xw(0, 1, 1, "S")
+            qt(3, 0)
+            tn(3, 1)
+            do(2, 0, 1, "S")
+            ai(0, 1, 0, "V")
+            tn(3, 2)
+            tc_(3, 1, "S")
+            dx(2, 1, 1)
+            ai(0, 1, 1, "V")
+            tc_(3, 2, "S")
+            dx(1, 1, 0)
+            qt(3, 1)
+            do(2, 1, 1, "S")
+            qa(0, 1)
+            xw(1, 1, 1, "S")
+            dx(2, 0, 0)
+            qt(3, 2)
+            ai(1, 1, 0, "V")
+            do(1, 1, 0, "S")
+            dx(3, 0, 1)
+            do(2, 0, 0, "S")
+            ai(1, 1, 1, "V")
+            xw(0, 1, 0, "S")
+            dx(3, 1, 1)
+            ai(1, 0, 0, "V")
+            do(3, 0, 1, "S")
+            qa(1, 1)
+            dx(2, 1, 0)
+            do(3, 1, 1, "S")
+            xi(0, 1, 0, "V")
+            xw(1, 1, 0, "S")
+            gv(0, 1)
+            xi(0, 1, 1, "V")
+            do(2, 1, 0, "S")
+            gv(1, 1)
+            xi(1, 1, 0, "S")
+            ev(0, 1)
+            gv(2, 1)
+            xq(0, 1)
+            gv(3, 1)
+            ev(1, 1)
+            xi(1, 1, 1, "S")
+            ev(2, 1)
+            dx(3, 0, 0)
+            ev(3, 1)
+            ai(0, 0, 1, "S")
+            dx(3, 1, 0)
+            xq(1, 1)
+            do(3, 0, 0, "V")
+            gv(4, 1)
+            do(3, 1, 0, "S")
+            qa(0, 0)
+            gv(5, 1)
+            ai(1, 0, 1, "S")
+            ev(4, 1)
+            gv(6, 1)
+            ev(5, 1)
+            gv(7, 1)
+            ai(0, 2, 0, "S")
+            qa(1, 0)
+            ev(6, 1)
+            gv(0, 0)
+            ai(0, 2, 1, "S")
+            ev(7, 1)
+            gv(1, 0)
+            ev(0, 0)
+            gv(2, 0)
+            ev(1, 0)
+            gv(3, 0)
+            ai(1, 2, 0, "S")
+            qa(0, 2)
+            gv(4, 0)
+            ev(2, 0)
+            ai(1, 2, 1, "S")
+            ev(3, 0)
+            gv(5, 0)
+            ev(4, 0)
+            gv(6, 0)
+            qa(1, 2)
+            gv(7, 0)
+            ev(5, 0)
+            ev(6, 0)
+            gv(0, 2)
+            ev(7, 0)
+            gv(1, 2)
+            ev(0, 2)
+            gv(2, 2)
+            ev(1, 2)
+            gv(3, 2)
+            ev(2, 2)
+            gv(4, 2)
+            ev(3, 2)
+            gv(5, 2)
+            ev(4, 2)
+            gv(6, 2)
+            ev(5, 2)
+            gv(7, 2)
+            ev(6, 2)
+            ev(7, 2)

@@ -45,7 +45,7 @@ def tile_gauss_newton_pullback_s8_kernel(tc, r, w2t, d, x_bytes, x_scale, w1t_wo
         w2_raw = [kept(f"w2_raw{h}", [P, 4, 512], BF16) for h in range(3)]
         d00 = kept("d00", [P, 2, 512], BF16)
         d01 = kept("d01", [P, 2, 1024], BF16)
-        d1, d2, d3 = [rolling("six", [P, 2, 1536], BF16, 5) for _ in range(3)]
+        d_raw = {s: rolling("six", [P, 2, 1536], BF16, 5) for s in range(1, 4)}
         v_raw = {}
         x_raw = [kept(f"x_raw{g}", [P, 4096], U8) for g in range(2)]
         x_sc = kept("x_sc", [P, 2, 4], F32)
@@ -75,19 +75,19 @@ def tile_gauss_newton_pullback_s8_kernel(tc, r, w2t, d, x_bytes, x_scale, w1t_wo
         load(r_raw[0][:], r_view[0][:, 0:2, :])
         load(d00[:], d_view[0][:, 0:2, 0:512])
         load(w2_raw[1][:], w2_view[:, :, 512:1024])
-        load(d01[:], d_view[0][:, 0:2, 512:1536])
-        load(w2_raw[2][:], w2_view[:, :, 1024:1536])
-        load(r_raw[1][:], r_view[0][:, 2:4, :])
-        load(d1[:], d_view[0][:, 2:4, :])
-        load(w1_words[:].bitcast(I32), w1t_words.bitcast(I32).rearrange("g p n -> p g n"))
-        w1_scale_load()
         load(x_sc[:], x_scale.rearrange("(g p t) o -> p g (t o)", p=P, t=4))
-        for g in range(2):
-            load(x_raw[g][:], x_view[g])
+        load(x_raw[0][:], x_view[0])
+        load(w2_raw[2][:], w2_view[:, :, 1024:1536])
+        load(d01[:], d_view[0][:, 0:2, 512:1536])
+        load(r_raw[1][:], r_view[0][:, 2:4, :])
+        load(x_raw[1][:], x_view[1])
+        load(d_raw[1][:], d_view[0][:, 2:4, :])
+        w1_scale_load()
+        load(w1_words[:].bitcast(I32), w1t_words.bitcast(I32).rearrange("g p n -> p g n"))
         load(r_raw[2][:], r_view[1])
         load(lam_rows[0:8, :], lam.rearrange("(k p) -> k p", p=P))
-        load(d2[:], d_view[1][:, 0:2, :])
-        load(d3[:], d_view[1][:, 2:4, :])
+        load(d_raw[2][:], d_view[1][:, 0:2, :])
+        load(d_raw[3][:], d_view[1][:, 2:4, :])
         load_v(0)
         load_v(1)
 
@@ -139,8 +139,8 @@ def tile_gauss_newton_pullback_s8_kernel(tc, r, w2t, d, x_bytes, x_scale, w1t_wo
 
         def wg(h, f, engine):
             if h not in w2i:
-                w2i[h] = rolling("w2i", [P, 512, 4], BF16, 2)
-            cols = slice(256 * f, 256 * (f + 1))
+                w2i[h] = rolling("interleaved", [P, 512, 4], BF16, 4)
+            cols = slice(256 * f, 256 * (f + 1)) if h == 0 else slice(0, 512)
             spread(engine, w2i[h][:, cols, :], w2_raw[h][:, :, cols].rearrange("c t f -> c f t"))
 
         def wq(h):
@@ -162,9 +162,7 @@ def tile_gauss_newton_pullback_s8_kernel(tc, r, w2t, d, x_bytes, x_scale, w1t_wo
         def d_row(s, h, e):
             if s == 0:
                 return d00[:, e, :] if h == 0 else d01[:, e, 512 * (h - 1) : 512 * h]
-            if s == 1:
-                return d1[:, e, 512 * h : 512 * (h + 1)]
-            return (d2 if s == 2 else d3)[:, e, 512 * h : 512 * (h + 1)]
+            return d_raw[s][:, e, 512 * h : 512 * (h + 1)]
 
         def m(s, h, e):
             g = s // 2
@@ -185,14 +183,22 @@ def tile_gauss_newton_pullback_s8_kernel(tc, r, w2t, d, x_bytes, x_scale, w1t_wo
                     nc.tensor.transpose(banks["t", s, h][:, 2 * e + u, :], words[:, P * u : P * (u + 1)], ident[:])
 
         def tc_(s, h, engine):
-            t_val[s, h] = rolling("t_val", [P, 1024], BF16, 4)
+            if h == 0:
+                t_val[s, 0] = rolling("t_val0", [P, 1, 1024], BF16, 2)
+            elif (s, 1) not in t_val:
+                t_val[s, 1] = rolling("t_val1", [P, 2, 1024], BF16, 2)
+            target = t_val[s, 0][:, 0, :] if h == 0 else t_val[s, 1][:, h - 1, :]
             copier(engine)(
-                out=t_val[s, h][:].bitcast(F32).rearrange("q (e p u) -> q e p u", e=2, u=2),
+                out=target.bitcast(F32).rearrange("q (e p u) -> q e p u", e=2, u=2),
                 in_=banks["t", s, h][:].rearrange("q (e u) p -> q e p u", u=2),
             )
 
-        def qt(s, h):
-            t_codes[s, h], t_scales[s, h] = quantize(f"t{s}{h}", t_val[s, h][:], 256)
+        def qt(s, part):
+            t_codes[s, part], t_scales[s, part] = quantize(f"t{s}{part}", t_val[s, part][:].rearrange("q h n -> q (h n)"), 256 * (part + 1))
+
+        def t_cols(h, e):
+            start = P * e if h < 2 else 256 + P * e
+            return slice(start, start + P)
 
         def dx(s, e, ih):
             bank = psum.tile([P, 512], F32, name="acc", tag="acc", bufs=3)
@@ -200,8 +206,8 @@ def tile_gauss_newton_pullback_s8_kernel(tc, r, w2t, d, x_bytes, x_scale, w1t_wo
             for h in range(3):
                 nc.tensor.matmul_mx(
                     out=bank[:],
-                    lhsT=t_codes[s, h][:, P * e : P * (e + 1)].bitcast(FP8X4),
-                    lhsT_scale=t_scales[s, h][:, P * e : P * (e + 1)],
+                    lhsT=t_codes[s, min(h, 1)][:, t_cols(h, e)].bitcast(FP8X4),
+                    lhsT_scale=t_scales[s, min(h, 1)][:, t_cols(h, e)],
                     rhs=w1_words[:, h, 1024 * ih : 1024 * (ih + 1)].bitcast(FP4X4),
                     rhs_scale=w1_scales[:, h, 512 * ih : 512 * (ih + 1)],
                     start=h == 0,
@@ -209,13 +215,17 @@ def tile_gauss_newton_pullback_s8_kernel(tc, r, w2t, d, x_bytes, x_scale, w1t_wo
                 )
 
         def do(s, e, ih, engine):
-            block = rolling("block", [P, 512], F32, 13)
-            copier(engine)(out=block[:], in_=banks["dx", s, e, ih][:])
-            nc.sync.dma_start(out=dx_view[s // 2][:, 2 * (s % 2) + e, 512 * ih : 512 * (ih + 1)], in_=block[:])
+            if (s, e) not in blocks:
+                blocks[s, e] = [rolling("block", [P, 1024], F32, 7), 0]
+            block = blocks[s, e]
+            copier(engine)(out=block[0][:, 512 * ih : 512 * (ih + 1)], in_=banks["dx", s, e, ih][:])
+            block[1] += 1
+            if block[1] == 2:
+                nc.sync.dma_start(out=dx_view[s // 2][:, 2 * (s % 2) + e, :], in_=block[0][:])
 
         def ai(g, h, u, engine):
             if (g, h) not in a_val:
-                a_val[g, h] = rolling("a_val", [P, 512, 4], BF16, 4)
+                a_val[g, h] = rolling("interleaved", [P, 512, 4], BF16, 4)
             spread(
                 engine,
                 a_val[g, h][:].rearrange("p (q u i) t -> p u q i t", u=2, i=2)[:, u],
@@ -225,27 +235,18 @@ def tile_gauss_newton_pullback_s8_kernel(tc, r, w2t, d, x_bytes, x_scale, w1t_wo
         def qa(g, h):
             a_codes[g, h], a_scales[g, h] = quantize(f"a{g}{h}", a_val[g, h][:].rearrange("p f t -> p (f t)"), 512)
 
-        def xw(g, ih, t, engine):
-            if (g, ih) not in wide:
-                wide[g, ih] = rolling("x_wide", [P, 4, 512], BF16, 4)
-            nc.scalar.activation(
-                out=wide[g, ih][:, t, :],
-                in_=x_raw[g][:, 1024 * t + 512 * ih : 1024 * t + 512 * (ih + 1)].bitcast(FP8),
-                func=COPY,
-                scale=x_sc[:, g, t : t + 1],
-            ) if engine == "S" else nc.vector.tensor_scalar(
-                out=wide[g, ih][:, t, :],
-                in0=x_raw[g][:, 1024 * t + 512 * ih : 1024 * t + 512 * (ih + 1)].bitcast(FP8),
-                scalar1=x_sc[:, g, t : t + 1],
-                scalar2=None,
-                op0=MULT,
-            )
+        def xw(g, t, engine):
+            if g not in wide:
+                wide[g] = rolling("x_wide", [P, 4, 1024], BF16, 2)
+            codes = x_raw[g][:, 1024 * t : 1024 * (t + 1)].bitcast(FP8)
+            if engine == "S":
+                nc.scalar.activation(out=wide[g][:, t, :], in_=codes, func=COPY, scale=x_sc[:, g, t : t + 1])
+            else:
+                nc.vector.tensor_scalar(out=wide[g][:, t, :], in0=codes, scalar1=x_sc[:, g, t : t + 1], scalar2=None, op0=MULT)
 
-        def xi(g, ih, f, engine):
-            if (g, ih) not in grouped:
-                grouped[g, ih] = rolling("x_grouped", [P, 512, 4], BF16, 2)
-            cols = slice(256 * f, 256 * (f + 1))
-            spread(engine, grouped[g, ih][:, cols, :], wide[g, ih][:, :, cols].rearrange("p t n -> p n t"))
+        def xi(g, ih, engine):
+            grouped[g, ih] = rolling("x_grouped", [P, 512, 4], BF16, 2)
+            spread(engine, grouped[g, ih][:], wide[g][:, :, 512 * ih : 512 * (ih + 1)].rearrange("p t n -> p n t"))
 
         def xq(g, ih):
             x_codes[g, ih], x_scales[g, ih] = quantize(f"x{g}{ih}", grouped[g, ih][:].rearrange("p n t -> p (n t)"), 512)
@@ -265,17 +266,34 @@ def tile_gauss_newton_pullback_s8_kernel(tc, r, w2t, d, x_bytes, x_scale, w1t_wo
                     stop=g == 1,
                 )
 
+        def gv_block(k, h):
+            part = (k, h) if k == 7 or h == 2 else (k, 0)
+            if ("gv",) + part not in blocks:
+                blocks[("gv",) + part] = [rolling("block", [P, 1024], F32, 7), 0]
+            return blocks[("gv",) + part]
+
+        def gv_store(k, h, block):
+            block[1] += 1
+            if k == 7 or h == 2:
+                nc.sync.dma_start(out=out_1[P * k : P * (k + 1), 512 * h : 512 * (h + 1)], in_=block[0][:, 0:512])
+            elif block[1] == 2:
+                nc.sync.dma_start(out=out_1[P * k : P * (k + 1), 0:1024], in_=block[0][:])
+
+        def gv_part(k, h):
+            col = 512 * h if k != 7 and h < 2 else 0
+            return slice(col, col + 512)
+
         def ev(k, h):
-            block = rolling("block", [P, 512], F32, 13)
+            block = gv_block(k, h)
             nc.vector.scalar_tensor_tensor(
-                out=block[:],
+                out=block[0][:, gv_part(k, h)],
                 in0=v_raw[k // 2][:, k % 2, 512 * h : 512 * (h + 1)],
                 scalar=lam32[:, k : k + 1],
                 in1=banks["gv", k, h][:],
                 op0=MULT,
                 op1=ADD,
             )
-            nc.sync.dma_start(out=out_1[P * k : P * (k + 1), 512 * h : 512 * (h + 1)], in_=block[:])
+            gv_store(k, h, block)
 
         def lv(k, h):
             blocks["l", k, h] = rolling("lam_v", [P, 512], F32, 3)
@@ -288,9 +306,9 @@ def tile_gauss_newton_pullback_s8_kernel(tc, r, w2t, d, x_bytes, x_scale, w1t_wo
             nc.scalar.copy(out=blocks["c", k, h][:], in_=banks["gv", k, h][:])
 
         def eg(k, h):
-            block = rolling("block", [P, 512], F32, 13)
-            nc.gpsimd.tensor_tensor(out=block[:], in0=blocks["c", k, h][:], in1=blocks["l", k, h][:], op=ADD)
-            nc.sync.dma_start(out=out_1[P * k : P * (k + 1), 512 * h : 512 * (h + 1)], in_=block[:])
+            block = gv_block(k, h)
+            nc.gpsimd.tensor_tensor(out=block[0][:, gv_part(k, h)], in0=blocks["c", k, h][:], in1=blocks["l", k, h][:], op=ADD)
+            gv_store(k, h, block)
 
         with tc.manual_schedule():
             lam_ident()
@@ -298,234 +316,216 @@ def tile_gauss_newton_pullback_s8_kernel(tc, r, w2t, d, x_bytes, x_scale, w1t_wo
             wg(0, 1, "S")
             rt(0)
             wq(0)
-            rc(0, "V")
+            rc(0, "S")
             rq(0)
-            wg(1, 1, "S")
+            s1(0, 0, 1)
             wg(1, 0, "V")
             s1(0, 0, 0)
-            s1(0, 0, 1)
-            m(0, 0, 0)
-            wq(1)
+            xw(0, 1, "S")
             m(0, 0, 1)
-            s1(0, 1, 0)
-            s1(0, 1, 1)
-            wg(2, 1, "S")
-            wg(2, 0, "V")
+            m(0, 0, 0)
+            xw(0, 3, "S")
+            wq(1)
             tn(0, 0)
-            rt(1)
-            m(0, 1, 0)
+            wg(2, 0, "V")
+            s1(0, 1, 0)
             tc_(0, 0, "S")
-            wq(2)
-            rc(1, "S")
+            s1(0, 1, 1)
+            xw(0, 0, "S")
             m(0, 1, 1)
+            rt(1)
+            wq(2)
+            xw(0, 2, "S")
+            m(0, 1, 0)
             s1(0, 2, 0)
-            s1(0, 2, 1)
-            rq(1)
-            tn(0, 1)
+            rc(1, "S")
             m(0, 2, 0)
-            tc_(0, 1, "S")
-            s1(1, 0, 0)
+            s1(0, 2, 1)
+            tn(0, 1)
+            xw(1, 2, "S")
+            xw(1, 3, "V")
+            qt(0, 0)
+            rq(1)
+            xw(1, 1, "S")
             m(0, 2, 1)
-            s1(1, 1, 0)
-            m(1, 0, 0)
             s1(1, 0, 1)
-            tn(0, 2)
-            m(1, 1, 0)
-            tc_(0, 2, "S")
-            s1(1, 2, 0)
+            s1(1, 1, 0)
             m(1, 0, 1)
+            tn(0, 2)
+            tc_(0, 1, "S")
+            m(1, 1, 0)
+            s1(1, 2, 0)
+            tc_(0, 2, "S")
             s1(1, 1, 1)
             m(1, 2, 0)
+            s1(1, 0, 0)
+            xi(0, 0, "S")
+            qt(0, 1)
             s1(1, 2, 1)
-            ai(0, 0, 0, "S")
-            tn(1, 0)
+            m(1, 0, 0)
+            dx(0, 0, 0)
             m(1, 1, 1)
-            tc_(1, 0, "V")
+            dx(0, 1, 1)
+            ai(0, 0, 0, "V")
+            do(0, 0, 0, "S")
+            xq(0, 0)
             tn(1, 1)
-            xw(0, 0, 3, "S")
-            qt(0, 0)
-            qt(1, 0)
+            tn(1, 0)
             tc_(1, 1, "S")
             m(1, 2, 1)
             load_v(2)
-            rt(2)
-            xw(1, 0, 3, "S")
-            qt(0, 1)
-            rt(3)
-            xw(0, 0, 2, "S")
-            rc(2, "V")
-            qt(1, 1)
-            rc(3, "S")
-            tn(1, 2)
-            rq(2)
-            xw(1, 0, 2, "S")
-            tc_(1, 2, "V")
-            lam_turn()
-            s1(2, 0, 0)
-            s1(2, 1, 0)
-            xw(0, 0, 1, "S")
-            rq(3)
-            s1(2, 0, 1)
-            lam_copy()
-            qt(0, 2)
-            xw(1, 0, 1, "S")
-            qt(1, 2)
             dx(0, 0, 1)
-            m(2, 0, 0)
-            xw(0, 0, 0, "S")
-            m(2, 1, 0)
-            s1(2, 2, 0)
-            do(0, 0, 1, "S")
-            dx(0, 1, 1)
-            m(2, 0, 1)
-            xw(1, 0, 0, "S")
-            m(2, 2, 0)
-            s1(3, 0, 0)
-            xi(0, 0, 0, "S")
-            tn(2, 0)
-            do(0, 1, 1, "V")
-            s1(2, 1, 1)
-            xi(1, 0, 0, "V")
-            s1(3, 1, 0)
-            tc_(2, 0, "S")
-            dx(1, 0, 1)
-            xi(1, 0, 1, "V")
-            xi(0, 0, 1, "S")
-            dx(1, 1, 1)
-            m(3, 0, 0)
-            xq(1, 0)
-            s1(2, 2, 1)
-            do(1, 0, 1, "S")
-            dx(0, 0, 0)
-            xq(0, 0)
-            do(1, 1, 1, "S")
-            qt(2, 0)
+            tc_(1, 0, "S")
+            ai(0, 1, 1, "V")
+            do(0, 1, 1, "S")
+            tn(1, 2)
+            qt(1, 0)
+            lam_turn()
+            ai(0, 2, 1, "V")
+            tc_(1, 2, "S")
             dx(0, 1, 0)
-            do(0, 0, 0, "S")
-            m(2, 1, 1)
-            xw(0, 1, 3, "S")
-            do(0, 1, 0, "V")
-            s1(3, 0, 1)
-            xw(1, 1, 3, "S")
-            tn(2, 1)
-            m(3, 1, 0)
-            tc_(2, 1, "S")
+            do(0, 0, 1, "S")
+            qt(1, 1)
+            rt(2)
+            do(0, 1, 0, "S")
+            lam_copy()
+            ai(0, 2, 0, "V")
+            rc(2, "S")
+            dx(1, 1, 1)
+            ai(0, 0, 1, "V")
+            ai(0, 1, 0, "S")
+            rt(3)
+            rq(2)
+            qa(0, 0)
+            s1(2, 1, 0)
+            do(1, 1, 1, "S")
+            s1(2, 0, 0)
+            qa(0, 1)
+            s1(2, 2, 0)
+            xw(1, 0, "S")
+            dx(1, 0, 1)
+            m(2, 0, 0)
+            m(2, 2, 0)
+            dx(1, 1, 0)
+            do(1, 0, 1, "S")
+            m(2, 1, 0)
+            xi(1, 0, "S")
+            rc(3, "V")
+            s1(2, 0, 1)
+            s1(2, 1, 1)
+            m(2, 0, 1)
+            s1(2, 2, 1)
             dx(1, 0, 0)
+            m(2, 1, 1)
+            rq(3)
+            tn(2, 1)
             m(2, 2, 1)
             load_v(3)
-            xw(0, 1, 2, "S")
-            qt(2, 1)
-            s1(3, 2, 0)
+            tc_(2, 1, "S")
+            s1(3, 1, 1)
+            xq(1, 0)
+            s1(3, 0, 1)
             do(1, 0, 0, "S")
+            s1(3, 0, 0)
             m(3, 0, 1)
             tn(2, 2)
-            tc_(2, 2, "S")
-            s1(3, 1, 1)
-            m(3, 2, 0)
-            tn(3, 0)
-            xw(1, 1, 2, "S")
-            qt(2, 2)
-            s1(3, 2, 1)
-            m(3, 1, 1)
-            tc_(3, 0, "S")
-            dx(2, 0, 1)
-            m(3, 2, 1)
-            xw(0, 1, 1, "S")
-            qt(3, 0)
-            tn(3, 1)
-            do(2, 0, 1, "S")
-            ai(0, 1, 0, "V")
-            tn(3, 2)
-            tc_(3, 1, "S")
-            dx(2, 1, 1)
-            ai(0, 1, 1, "V")
-            tc_(3, 2, "S")
-            dx(1, 1, 0)
-            qt(3, 1)
-            do(2, 1, 1, "S")
-            qa(0, 1)
-            xw(1, 1, 1, "S")
-            dx(2, 0, 0)
-            qt(3, 2)
-            ai(1, 1, 0, "V")
             do(1, 1, 0, "S")
-            dx(3, 0, 1)
-            do(2, 0, 0, "S")
-            ai(1, 1, 1, "V")
-            xw(0, 1, 0, "S")
-            dx(3, 1, 1)
-            ai(1, 0, 0, "V")
-            do(3, 0, 1, "S")
-            qa(1, 1)
-            dx(2, 1, 0)
-            do(3, 1, 1, "S")
-            xi(0, 1, 0, "V")
-            xw(1, 1, 0, "S")
-            gv(0, 1)
-            xi(0, 1, 1, "V")
-            do(2, 1, 0, "S")
-            gv(1, 1)
-            xi(1, 1, 0, "S")
-            ev(0, 1)
-            gv(2, 1)
-            xq(0, 1)
-            gv(3, 1)
-            ev(1, 1)
-            xi(1, 1, 1, "S")
-            ev(2, 1)
-            dx(3, 0, 0)
-            ev(3, 1)
-            ai(0, 0, 1, "S")
-            dx(3, 1, 0)
-            xq(1, 1)
-            do(3, 0, 0, "V")
-            gv(4, 1)
-            do(3, 1, 0, "S")
-            qa(0, 0)
-            gv(5, 1)
+            tn(2, 0)
+            m(3, 1, 1)
+            tc_(2, 2, "S")
+            m(3, 0, 0)
+            s1(3, 1, 0)
+            tc_(2, 0, "S")
+            s1(3, 2, 1)
+            qt(2, 1)
             ai(1, 0, 1, "S")
-            ev(4, 1)
-            gv(6, 1)
-            ev(5, 1)
-            gv(7, 1)
-            ai(0, 2, 0, "S")
+            tn(3, 0)
+            qt(2, 0)
+            s1(3, 2, 0)
+            m(3, 1, 0)
+            dx(2, 1, 1)
+            tc_(3, 0, "S")
+            m(3, 2, 0)
+            dx(2, 0, 1)
+            do(2, 1, 1, "S")
+            ai(1, 1, 1, "V")
+            ai(1, 0, 0, "S")
+            ai(1, 1, 0, "V")
+            dx(2, 1, 0)
+            m(3, 2, 1)
+            dx(2, 0, 0)
+            do(2, 1, 0, "S")
             qa(1, 0)
-            ev(6, 1)
-            gv(0, 0)
-            ai(0, 2, 1, "S")
-            ev(7, 1)
-            gv(1, 0)
-            ev(0, 0)
-            gv(2, 0)
-            ev(1, 0)
-            gv(3, 0)
-            ai(1, 2, 0, "S")
+            do(2, 0, 1, "S")
+            tn(3, 2)
+            qa(1, 1)
+            tn(3, 1)
+            do(2, 0, 0, "S")
             qa(0, 2)
-            gv(4, 0)
-            ev(2, 0)
+            gv(1, 0)
+            tc_(3, 2, "S")
+            qt(3, 0)
+            gv(1, 1)
             ai(1, 2, 1, "S")
+            ev(1, 0)
+            gv(0, 1)
+            ev(1, 1)
+            gv(2, 1)
+            ev(0, 1)
+            ai(1, 2, 0, "S")
+            gv(0, 0)
+            ev(2, 1)
+            gv(2, 0)
+            ev(0, 0)
+            tc_(3, 1, "S")
+            gv(3, 1)
+            ev(2, 0)
+            xi(1, 1, "S")
+            gv(3, 0)
+            qt(3, 1)
+            ev(3, 1)
+            dx(3, 0, 1)
             ev(3, 0)
-            gv(5, 0)
-            ev(4, 0)
-            gv(6, 0)
+            dx(3, 0, 0)
             qa(1, 2)
-            gv(7, 0)
-            ev(5, 0)
-            ev(6, 0)
-            gv(0, 2)
-            ev(7, 0)
-            gv(1, 2)
-            ev(0, 2)
+            do(3, 0, 1, "S")
+            xq(1, 1)
             gv(2, 2)
+            do(3, 0, 0, "S")
+            gv(1, 2)
+            ev(2, 2)
+            xi(0, 1, "S")
+            gv(0, 2)
             ev(1, 2)
             gv(3, 2)
-            ev(2, 2)
-            gv(4, 2)
+            ev(0, 2)
+            dx(3, 1, 0)
             ev(3, 2)
+            dx(3, 1, 1)
+            do(3, 1, 0, "S")
+            xq(0, 1)
             gv(5, 2)
-            ev(4, 2)
-            gv(6, 2)
+            do(3, 1, 1, "S")
+            gv(6, 1)
             ev(5, 2)
             gv(7, 2)
-            ev(6, 2)
+            ev(6, 1)
+            gv(4, 2)
             ev(7, 2)
+            gv(6, 0)
+            ev(4, 2)
+            gv(5, 1)
+            ev(6, 0)
+            gv(6, 2)
+            ev(5, 1)
+            gv(5, 0)
+            ev(6, 2)
+            gv(4, 0)
+            ev(5, 0)
+            gv(7, 1)
+            ev(4, 0)
+            gv(4, 1)
+            ev(7, 1)
+            gv(7, 0)
+            ev(4, 1)
+            ev(7, 0)

@@ -56,6 +56,9 @@ def tile_gauss_newton_pullback_s8_kernel(tc, r, w2t, d, x_bytes, x_scale, w1t_wo
         ident = kept("ident", [P, P], F32)
         ident16 = kept("ident16", [P, P], BF16)
 
+        warm_tile = kept("warm_tile", [P, 512], BF16)
+        nc.vector.memset(warm_tile[:], 0)
+        warm_bank = psum.tile([P, 512], F32, name="acc", tag="acc", bufs=3)
         make_identity(nc, ident[:])
         nc.gpsimd.memset(lam_rows[:], 0)
         nc.gpsimd.memset(w1_scales[:].rearrange("p g n -> p (g n)").bitcast(I32), 0)
@@ -119,6 +122,10 @@ def tile_gauss_newton_pullback_s8_kernel(tc, r, w2t, d, x_bytes, x_scale, w1t_wo
 
         def lam_copy():
             nc.vector.tensor_copy(out=lam32[:], in_=banks["lam"][:, 0:8])
+
+        def warm(count):
+            for _ in range(count):
+                nc.tensor.matmul(warm_bank[:], lhsT=warm_tile[:, 0:P], rhs=warm_tile[:], start=True, stop=True)
 
         def rt(s):
             banks["r", s] = psum.tile([P, 4, P], F32, name="turned", tag="turned", bufs=2)
@@ -311,16 +318,19 @@ def tile_gauss_newton_pullback_s8_kernel(tc, r, w2t, d, x_bytes, x_scale, w1t_wo
             gv_store(k, h, block)
 
         with tc.manual_schedule():
+            warm(4)
             lam_ident()
             wg(0, 0, "V")
             wg(0, 1, "S")
             rt(0)
+            warm(3)
             wq(0)
             rc(0, "S")
             rq(0)
             s1(0, 0, 1)
             wg(1, 0, "V")
             s1(0, 0, 0)
+            warm(5)
             xw(0, 1, "S")
             m(0, 0, 1)
             m(0, 0, 0)
@@ -334,10 +344,12 @@ def tile_gauss_newton_pullback_s8_kernel(tc, r, w2t, d, x_bytes, x_scale, w1t_wo
             xw(0, 0, "S")
             m(0, 1, 1)
             rt(1)
+            warm(3)
             wq(2)
             xw(0, 2, "S")
             m(0, 1, 0)
             s1(0, 2, 0)
+            warm(2)
             rc(1, "S")
             m(0, 2, 0)
             s1(0, 2, 1)

from contextlib import ExitStack

import concourse.mybir as mybir
from concourse.masks import make_identity

M, C, F, I = 1024, 512, 1536, 1024
FLOPS = 2 * M * C * F + 2 * M * F * I + 2 * I * M * F

F32 = mybir.dt.float32
BF16 = mybir.dt.bfloat16
I32 = mybir.dt.int32
U32 = mybir.dt.uint32
U8 = mybir.dt.uint8
FP8 = mybir.dt.float8_e4m3fn
FP8X4 = mybir.dt.float8_e4m3fn_x4
FP4X4 = mybir.dt.float4_e2m1fn_x4
MULT = mybir.AluOpType.mult
ADD = mybir.AluOpType.add
COPY = mybir.ActivationFunctionType.Copy

P = 128


def tile_gauss_newton_pullback_s8_kernel(tc, r, w2t, d, x_bytes, x_scale, w1t_words, w1t_scales, v, lam, out_0, out_1):
    nc = tc.nc
    with ExitStack() as ctx:
        keep = ctx.enter_context(tc.tile_pool(name="keep", bufs=1))
        work = ctx.enter_context(tc.tile_pool(name="work", bufs=2))
        psum = ctx.enter_context(tc.psum_pool(name="psum", bufs=2))

        def kept(name, shape, dtype):
            return keep.tile(shape, dtype, name=name, tag=name, bufs=1, align_bytes=64)

        def rolling(name, shape, dtype, bufs):
            return work.tile(shape, dtype, name=name, tag=name, bufs=bufs, align_bytes=64)

        r_view = r.rearrange("(g p t) c -> g p t c", p=P, t=4)
        w2_view = w2t.rearrange("(p t) f -> p t f", t=4)
        d_view = d.rearrange("(g p t) f -> g p t f", p=P, t=4)
        x_view = x_bytes.rearrange("(g p t) n -> g p (t n)", p=P, t=4)
        v_view = v.rearrange("(a k p) f -> a p k f", p=P, k=2)
        dx_view = out_0.rearrange("(g p t) i -> g p t i", p=P, t=4)

        r_raw = [kept("r_raw0", [P, 2, 512], BF16), kept("r_raw1", [P, 2, 512], BF16), kept("r_raw23", [P, 4, 512], BF16)]
        w2_raw = [kept(f"w2_raw{h}", [P, 4, 512], BF16) for h in range(3)]
        d00 = kept("d00", [P, 2, 512], BF16)
        d01 = kept("d01", [P, 2, 1024], BF16)
        d_raw = {s: rolling("six", [P, 2, 1536], BF16, 5) for s in range(1, 4)}
        v_raw = {}
        x_raw = [kept(f"x_raw{g}", [P, 4096], U8) for g in range(2)]
        x_sc = kept("x_sc", [P, 2, 4], F32)
        w1_words = kept("w1_words", [P, 3, 2048], U8)
        w1_scales = kept("w1_scales", [P, 3, 1024], U8)
        lam_rows = kept("lam_rows", [P, P], BF16)
        lam32 = kept("lam32", [P, 8], F32)
        ident = kept("ident", [P, P], F32)
        ident16 = kept("ident16", [P, P], BF16)

        warm_tile = kept("warm_tile", [P, 512], BF16)
        nc.vector.memset(warm_tile[:], 0)
        warm_bank = psum.tile([P, 512], F32, name="acc", tag="acc", bufs=3)
        make_identity(nc, ident[:])
        nc.gpsimd.memset(lam_rows[:], 0)
        nc.gpsimd.memset(w1_scales[:].rearrange("p g n -> p (g n)").bitcast(I32), 0)

        def load(tile, source):
            nc.sync.dma_start(out=tile, in_=source)

        def load_v(a):
            v_raw[a] = rolling("six", [P, 2, 1536], BF16, 5)
            load(v_raw[a][:], v_view[a])

        def w1_scale_load():
            for quad in range(4):
                load(w1_scales[32 * quad : 32 * quad + 4, :, :].bitcast(I32), w1t_scales.bitcast(I32).rearrange("g s n -> s g n")[4 * quad : 4 * quad + 4])

        load(w2_raw[0][:], w2_view[:, :, 0:512])
        load(r_raw[0][:], r_view[0][:, 0:2, :])
        load(d00[:], d_view[0][:, 0:2, 0:512])
        load(w2_raw[1][:], w2_view[:, :, 512:1024])
        load(x_sc[:], x_scale.rearrange("(g p t) o -> p g (t o)", p=P, t=4))
        load(x_raw[0][:], x_view[0])
        load(w2_raw[2][:], w2_view[:, :, 1024:1536])
        load(d01[:], d_view[0][:, 0:2, 512:1536])
        load(r_raw[1][:], r_view[0][:, 2:4, :])
        load(x_raw[1][:], x_view[1])
        load(d_raw[1][:], d_view[0][:, 2:4, :])
        w1_scale_load()
        load(w1_words[:].bitcast(I32), w1t_words.bitcast(I32).rearrange("g p n -> p g n"))
        load(r_raw[2][:], r_view[1])
        load(lam_rows[0:8, :], lam.rearrange("(k p) -> k p", p=P))
        load(d_raw[2][:], d_view[1][:, 0:2, :])
        load(d_raw[3][:], d_view[1][:, 2:4, :])
        load_v(0)
        load_v(1)

        r_codes, r_scales, w2_codes, w2_scales = {}, {}, {}, {}
        a_codes, a_scales, t_codes, t_scales, x_codes, x_scales = {}, {}, {}, {}, {}, {}
        rt_val, w2i, b_val, a_val, t_val, wide, grouped, banks, blocks = {}, {}, {}, {}, {}, {}, {}, {}, {}

        def quantize(name, value, width):
            codes = kept(name + "_c", [P, width], U32)
            scales = kept(name + "_s", [P, width], U8)
            nc.vector.quantize_mx(out=codes[:].bitcast(FP8X4), scales=scales[:], in_=value)
            return codes, scales

        def copier(engine):
            return nc.scalar.copy if engine == "S" else nc.vector.tensor_copy

        def spread(engine, out, in_):
            if engine == "G":
                nc.gpsimd.tensor_scalar(out=out, in0=in_, scalar1=1.0, scalar2=0.0, op0=MULT, op1=ADD)
            else:
                copier(engine)(out=out, in_=in_)

        def lam_ident():
            nc.vector.tensor_copy(out=ident16[:], in_=ident[:])

        def lam_turn():
            bank = banks["lam"] = psum.tile([P, P], BF16, name="turned", tag="turned", bufs=2)
            nc.tensor.transpose(bank[:], lam_rows[:], ident16[:])

        def lam_copy():
            nc.vector.tensor_copy(out=lam32[:], in_=banks["lam"][:, 0:8])

        def warm(count):
            for _ in range(count):
                nc.tensor.matmul(warm_bank[:], lhsT=warm_tile[:, 0:P], rhs=warm_tile[:], start=True, stop=True)

        def rt(s):
            banks["r", s] = psum.tile([P, 4, P], F32, name="turned", tag="turned", bufs=2)
            for e in range(2):
                raw = r_raw[s][:, e, :] if s < 2 else r_raw[2][:, 2 * (s - 2) + e, :]
                for u in range(2):
                    nc.tensor.transpose(banks["r", s][:, 2 * e + u, :], raw.bitcast(F32)[:, u:256:2], ident[:])

        def rc(s, engine):
            rt_val[s] = rolling("rt_val", [P, 1024], BF16, 2)
            copier(engine)(
                out=rt_val[s][:].bitcast(F32).rearrange("q (e p u) -> q e p u", e=2, u=2),
                in_=banks["r", s][:].rearrange("q (e u) p -> q e p u", u=2),
            )

        def rq(s):
            r_codes[s], r_scales[s] = quantize(f"r{s}", rt_val[s][:], 256)

        def wg(h, f, engine):
            if h not in w2i:
                w2i[h] = rolling("interleaved", [P, 512, 4], BF16, 4)
            cols = slice(256 * f, 256 * (f + 1)) if h == 0 else slice(0, 512)
            spread(engine, w2i[h][:, cols, :], w2_raw[h][:, :, cols].rearrange("c t f -> c f t"))

        def wq(h):
            w2_codes[h], w2_scales[h] = quantize(f"w2{h}", w2i[h][:].rearrange("c f t -> c (f t)"), 512)

        def s1(s, h, e):
            banks["s1", s, h, e] = psum.tile([P, 512], F32, name="s1", tag="s1", bufs=3)
            cols = slice(P * e, P * (e + 1))
            nc.tensor.matmul_mx(
                out=banks["s1", s, h, e][:],
                lhsT=r_codes[s][:, cols].bitcast(FP8X4),
                lhsT_scale=r_scales[s][:, cols],
                rhs=w2_codes[h][:].bitcast(FP8X4),
                rhs_scale=w2_scales[h][:],
                start=True,
                stop=True,
            )

        def d_row(s, h, e):
            if s == 0:
                return d00[:, e, :] if h == 0 else d01[:, e, 512 * (h - 1) : 512 * h]
            return d_raw[s][:, e, 512 * h : 512 * (h + 1)]

        def m(s, h, e):
            g = s // 2
            if (g, h) not in b_val:
                b_val[g, h] = rolling("b_val", [P, 4, 512], BF16, 6)
            nc.vector.tensor_tensor(
                out=b_val[g, h][:, 2 * (s % 2) + e, :].rearrange("p (u q i) -> p u q i", u=2, i=2),
                in0=banks["s1", s, h, e][:].rearrange("p (q u i) -> p u q i", u=2, i=2),
                in1=d_row(s, h, e).rearrange("p (q u i) -> p u q i", u=2, i=2),
                op=MULT,
            )

        def tn(s, h):
            banks["t", s, h] = psum.tile([P, 4, P], F32, name="turned", tag="turned", bufs=2)
            for e in range(2):
                words = b_val[s // 2, h][:, 2 * (s % 2) + e, :].bitcast(F32)
                for u in range(2):
                    nc.tensor.transpose(banks["t", s, h][:, 2 * e + u, :], words[:, P * u : P * (u + 1)], ident[:])

        def tc_(s, h, engine):
            if h == 0:
                t_val[s, 0] = rolling("t_val0", [P, 1, 1024], BF16, 2)
            elif (s, 1) not in t_val:
                t_val[s, 1] = rolling("t_val1", [P, 2, 1024], BF16, 2)
            target = t_val[s, 0][:, 0, :] if h == 0 else t_val[s, 1][:, h - 1, :]
            copier(engine)(
                out=target.bitcast(F32).rearrange("q (e p u) -> q e p u", e=2, u=2),
                in_=banks["t", s, h][:].rearrange("q (e u) p -> q e p u", u=2),
            )

        def qt(s, part):
            t_codes[s, part], t_scales[s, part] = quantize(f"t{s}{part}", t_val[s, part][:].rearrange("q h n -> q (h n)"), 256 * (part + 1))

        def t_cols(h, e):
            start = P * e if h < 2 else 256 + P * e
            return slice(start, start + P)

        def dx(s, e, ih):
            bank = psum.tile([P, 512], F32, name="acc", tag="acc", bufs=3)
            banks["dx", s, e, ih] = bank
            for h in range(3):
                nc.tensor.matmul_mx(
                    out=bank[:],
                    lhsT=t_codes[s, min(h, 1)][:, t_cols(h, e)].bitcast(FP8X4),
                    lhsT_scale=t_scales[s, min(h, 1)][:, t_cols(h, e)],
                    rhs=w1_words[:, h, 1024 * ih : 1024 * (ih + 1)].bitcast(FP4X4),
                    rhs_scale=w1_scales[:, h, 512 * ih : 512 * (ih + 1)],
                    start=h == 0,
                    stop=h == 2,
                )

        def do(s, e, ih, engine):
            if (s, e) not in blocks:
                blocks[s, e] = [rolling("block", [P, 1024], F32, 7), 0]
            block = blocks[s, e]
            copier(engine)(out=block[0][:, 512 * ih : 512 * (ih + 1)], in_=banks["dx", s, e, ih][:])
            block[1] += 1
            if block[1] == 2:
                nc.sync.dma_start(out=dx_view[s // 2][:, 2 * (s % 2) + e, :], in_=block[0][:])

        def ai(g, h, u, engine):
            if (g, h) not in a_val:
                a_val[g, h] = rolling("interleaved", [P, 512, 4], BF16, 4)
            spread(
                engine,
                a_val[g, h][:].rearrange("p (q u i) t -> p u q i t", u=2, i=2)[:, u],
                b_val[g, h][:].rearrange("p t (u q i) -> p u q i t", u=2, i=2)[:, u],
            )

        def qa(g, h):
            a_codes[g, h], a_scales[g, h] = quantize(f"a{g}{h}", a_val[g, h][:].rearrange("p f t -> p (f t)"), 512)

        def xw(g, t, engine):
            if g not in wide:
                wide[g] = rolling("x_wide", [P, 4, 1024], BF16, 2)
            codes = x_raw[g][:, 1024 * t : 1024 * (t + 1)].bitcast(FP8)
            if engine == "S":
                nc.scalar.activation(out=wide[g][:, t, :], in_=codes, func=COPY, scale=x_sc[:, g, t : t + 1])
            else:
                nc.vector.tensor_scalar(out=wide[g][:, t, :], in0=codes, scalar1=x_sc[:, g, t : t + 1], scalar2=None, op0=MULT)

        def xi(g, ih, engine):
            grouped[g, ih] = rolling("x_grouped", [P, 512, 4], BF16, 2)
            spread(engine, grouped[g, ih][:], wide[g][:, :, 512 * ih : 512 * (ih + 1)].rearrange("p t n -> p n t"))

        def xq(g, ih):
            x_codes[g, ih], x_scales[g, ih] = quantize(f"x{g}{ih}", grouped[g, ih][:].rearrange("p n t -> p (n t)"), 512)

        def gv(k, h):
            ih, cols = k // 4, slice(P * (k % 4), P * (k % 4 + 1))
            bank = psum.tile([P, 512], F32, name="acc", tag="acc", bufs=3)
            banks["gv", k, h] = bank
            for g in range(2):
                nc.tensor.matmul_mx(
                    out=bank[:],
                    lhsT=x_codes[g, ih][:, cols].bitcast(FP8X4),
                    lhsT_scale=x_scales[g, ih][:, cols],
                    rhs=a_codes[g, h][:].bitcast(FP8X4),
                    rhs_scale=a_scales[g, h][:],
                    start=g == 0,
                    stop=g == 1,
                )

        def gv_block(k, h):
            part = (k, h) if k == 7 or h == 2 else (k, 0)
            if ("gv",) + part not in blocks:
                blocks[("gv",) + part] = [rolling("block", [P, 1024], F32, 7), 0]
            return blocks[("gv",) + part]

        def gv_store(k, h, block):
            block[1] += 1
            if k == 7 or h == 2:
                nc.sync.dma_start(out=out_1[P * k : P * (k + 1), 512 * h : 512 * (h + 1)], in_=block[0][:, 0:512])
            elif block[1] == 2:
                nc.sync.dma_start(out=out_1[P * k : P * (k + 1), 0:1024], in_=block[0][:])

        def gv_part(k, h):
            col = 512 * h if k != 7 and h < 2 else 0
            return slice(col, col + 512)

        def ev(k, h):
            block = gv_block(k, h)
            nc.vector.scalar_tensor_tensor(
                out=block[0][:, gv_part(k, h)],
                in0=v_raw[k // 2][:, k % 2, 512 * h : 512 * (h + 1)],
                scalar=lam32[:, k : k + 1],
                in1=banks["gv", k, h][:],
                op0=MULT,
                op1=ADD,
            )
            gv_store(k, h, block)

        def lv(k, h):
            blocks["l", k, h] = rolling("lam_v", [P, 512], F32, 3)
            nc.scalar.activation(
                out=blocks["l", k, h][:], in_=v_raw[k // 2][:, k % 2, 512 * h : 512 * (h + 1)], func=COPY, scale=lam32[:, k : k + 1]
            )

        def ec(k, h):
            blocks["c", k, h] = rolling("gv_copy", [P, 512], F32, 3)
            nc.scalar.copy(out=blocks["c", k, h][:], in_=banks["gv", k, h][:])

        def eg(k, h):
            block = gv_block(k, h)
            nc.gpsimd.tensor_tensor(out=block[0][:, gv_part(k, h)], in0=blocks["c", k, h][:], in1=blocks["l", k, h][:], op=ADD)
            gv_store(k, h, block)

        with tc.manual_schedule():
            warm(4)
            lam_ident()
            wg(0, 0, "V")
            wg(0, 1, "S")
            rt(0)
            warm(3)
            wq(0)
            rc(0, "S")
            rq(0)
            s1(0, 0, 1)
            wg(1, 0, "V")
            s1(0, 0, 0)
            warm(5)
            xw(0, 1, "S")
            m(0, 0, 1)
            m(0, 0, 0)
            xw(0, 3, "S")
            wq(1)
            tn(0, 0)
            wg(2, 0, "V")
            s1(0, 1, 0)
            tc_(0, 0, "S")
            s1(0, 1, 1)
            xw(0, 0, "S")
            m(0, 1, 1)
            rt(1)
            warm(3)
            wq(2)
            xw(0, 2, "S")
            m(0, 1, 0)
            s1(0, 2, 0)
            warm(2)
            rc(1, "S")
            m(0, 2, 0)
            s1(0, 2, 1)
            tn(0, 1)
            xw(1, 2, "S")
            xw(1, 3, "V")
            qt(0, 0)
            rq(1)
            xw(1, 1, "S")
            m(0, 2, 1)
            s1(1, 0, 1)
            s1(1, 1, 0)
            m(1, 0, 1)
            tn(0, 2)
            tc_(0, 1, "S")
            m(1, 1, 0)
            s1(1, 2, 0)
            tc_(0, 2, "S")
            s1(1, 1, 1)
            m(1, 2, 0)
            s1(1, 0, 0)
            xi(0, 0, "S")
            qt(0, 1)
            s1(1, 2, 1)
            m(1, 0, 0)
            dx(0, 0, 0)
            m(1, 1, 1)
            dx(0, 1, 1)
            ai(0, 0, 0, "V")
            do(0, 0, 0, "S")
            xq(0, 0)
            tn(1, 1)
            tn(1, 0)
            tc_(1, 1, "S")
            m(1, 2, 1)
            load_v(2)
            dx(0, 0, 1)
            tc_(1, 0, "S")
            ai(0, 1, 1, "V")
            do(0, 1, 1, "S")
            tn(1, 2)
            qt(1, 0)
            lam_turn()
            ai(0, 2, 1, "V")
            tc_(1, 2, "S")
            dx(0, 1, 0)
            do(0, 0, 1, "S")
            qt(1, 1)
            rt(2)
            do(0, 1, 0, "S")
            lam_copy()
            ai(0, 2, 0, "V")
            rc(2, "S")
            dx(1, 1, 1)
            ai(0, 0, 1, "V")
            ai(0, 1, 0, "S")
            rt(3)
            rq(2)
            qa(0, 0)
            s1(2, 1, 0)
            do(1, 1, 1, "S")
            s1(2, 0, 0)
            qa(0, 1)
            s1(2, 2, 0)
            xw(1, 0, "S")
            dx(1, 0, 1)
            m(2, 0, 0)
            m(2, 2, 0)
            dx(1, 1, 0)
            do(1, 0, 1, "S")
            m(2, 1, 0)
            xi(1, 0, "S")
            rc(3, "V")
            s1(2, 0, 1)
            s1(2, 1, 1)
            m(2, 0, 1)
            s1(2, 2, 1)
            dx(1, 0, 0)
            m(2, 1, 1)
            rq(3)
            tn(2, 1)
            m(2, 2, 1)
            load_v(3)
            tc_(2, 1, "S")
            s1(3, 1, 1)
            xq(1, 0)
            s1(3, 0, 1)
            do(1, 0, 0, "S")
            s1(3, 0, 0)
            m(3, 0, 1)
            tn(2, 2)
            do(1, 1, 0, "S")
            tn(2, 0)
            m(3, 1, 1)
            tc_(2, 2, "S")
            m(3, 0, 0)
            s1(3, 1, 0)
            tc_(2, 0, "S")
            s1(3, 2, 1)
            qt(2, 1)
            ai(1, 0, 1, "S")
            tn(3, 0)
            qt(2, 0)
            s1(3, 2, 0)
            m(3, 1, 0)
            dx(2, 1, 1)
            tc_(3, 0, "S")
            m(3, 2, 0)
            dx(2, 0, 1)
            do(2, 1, 1, "S")
            ai(1, 1, 1, "V")
            ai(1, 0, 0, "S")
            ai(1, 1, 0, "V")
            dx(2, 1, 0)
            m(3, 2, 1)
            dx(2, 0, 0)
            do(2, 1, 0, "S")
            qa(1, 0)
            do(2, 0, 1, "S")
            tn(3, 2)
            qa(1, 1)
            tn(3, 1)
            do(2, 0, 0, "S")
            qa(0, 2)
            gv(1, 0)
            tc_(3, 2, "S")
            qt(3, 0)
            gv(1, 1)
            ai(1, 2, 1, "S")
            ev(1, 0)
            gv(0, 1)
            ev(1, 1)
            gv(2, 1)
            ev(0, 1)
            ai(1, 2, 0, "S")
            gv(0, 0)
            ev(2, 1)
            gv(2, 0)
            ev(0, 0)
            tc_(3, 1, "S")
            gv(3, 1)
            ev(2, 0)
            xi(1, 1, "S")
            gv(3, 0)
            qt(3, 1)
            ev(3, 1)
            dx(3, 0, 1)
            ev(3, 0)
            dx(3, 0, 0)
            qa(1, 2)
            do(3, 0, 1, "S")
            xq(1, 1)
            gv(2, 2)
            do(3, 0, 0, "S")
            gv(1, 2)
            ev(2, 2)
            xi(0, 1, "S")
            gv(0, 2)
            ev(1, 2)
            gv(3, 2)
            ev(0, 2)
            dx(3, 1, 0)
            ev(3, 2)
            dx(3, 1, 1)
            do(3, 1, 0, "S")
            xq(0, 1)
            gv(5, 2)
            do(3, 1, 1, "S")
            gv(6, 1)
            ev(5, 2)
            gv(7, 2)
            ev(6, 1)
            gv(4, 2)
            ev(7, 2)
            gv(6, 0)
            ev(4, 2)
            gv(5, 1)
            ev(6, 0)
            gv(6, 2)
            ev(5, 1)
            gv(5, 0)
            ev(6, 2)
            gv(4, 0)
            ev(5, 0)
            gv(7, 1)
            ev(4, 0)
            gv(4, 1)
            ev(7, 1)
            gv(7, 0)
            ev(4, 1)
            ev(7, 0)
